import numpy as np
import ml_dtypes


def mxq(x, axis, fmt="e4m3"):
    dtype, down = {"e4m3": (ml_dtypes.float8_e4m3fn, 7), "e5m2": (ml_dtypes.float8_e5m2, 14)}[fmt]
    v = np.moveaxis(np.asarray(x, np.float32).astype(ml_dtypes.bfloat16).astype(np.float64), axis, -1)
    blocks = v.reshape(v.shape[:-1] + (-1, 32))
    amax = np.abs(blocks).max(-1, keepdims=True)
    byte = np.maximum(np.where(amax > 0, np.frexp(amax)[1] - 1 + 127, 0) - down, 1)
    scale = np.exp2(byte - 127.0)
    codes = (blocks / scale).astype(np.float32).astype(dtype).astype(np.float64)
    return np.moveaxis((codes * scale).reshape(v.shape), -1, axis)


WIDE = False


def mx_kscale(k):
    if not WIDE:
        return np.ones(k)
    levels = np.array([10, -10, 5, -5, 0])
    if k % 512:
        return np.exp2(np.random.permutation(np.resize(levels, k // 32))).repeat(32)
    a = np.empty((k // 512, 16))
    for p in range(k // 512):
        a[p, :8] = np.random.permutation(np.resize(levels, 8))
        for g in range(8):
            far = levels[np.abs(levels - a[p, g]) >= 10]
            a[p, g + 8] = far[np.random.randint(len(far))]
    return np.exp2(a.ravel()).repeat(32)


BF16 = ml_dtypes.bfloat16


def bf(x):
    return np.asarray(x, np.float32).astype(BF16)


def f64(x):
    return np.asarray(x).astype(np.float64)


E2M1 = np.array([0.0, 0.5, 1.0, 1.5, 2.0, 3.0, 4.0, 6.0, -0.0, -0.5, -1.0, -1.5, -2.0, -3.0, -4.0, -6.0])


def pack_weight(w, fmt):
    k, n = w.shape
    w = f64(bf(w)).reshape(k // 32, 32, n)
    amax = np.abs(w).max(1)
    if fmt == "e4m3":
        byte = np.frexp(amax)[1] - 1 + 127 - 7
    else:
        mant, ex = np.frexp(amax / 6.0)
        byte = np.where(mant > 0.5, ex, ex - 1) + 127
    byte = np.clip(np.where(amax > 0, byte, 1), 1, 254)
    scaled = (w * np.exp2(127.0 - byte)[:, None, :]).reshape(k, n).astype(np.float32)
    by_word = np.ascontiguousarray(scaled.reshape(k // 512, 128, 4, n).transpose(0, 1, 3, 2))
    if fmt == "e4m3":
        words = by_word.astype(ml_dtypes.float8_e4m3fn).view(np.uint8)
    else:
        c = by_word.astype(ml_dtypes.float4_e2m1fn).view(np.uint8) & 0xF
        words = c[..., 0::2] | (c[..., 1::2] << 4)
    return np.ascontiguousarray(words), np.ascontiguousarray(byte.astype(np.uint8).reshape(k // 512, 16, n))


def unpack_weight(words, scales, fmt):
    g, p, n, _ = words.shape
    if fmt == "e4m3":
        vals = np.ascontiguousarray(words).view(ml_dtypes.float8_e4m3fn).astype(np.float64)
    else:
        nib = np.empty((g, p, n, 4), np.uint8)
        nib[..., 0::2] = words & 0xF
        nib[..., 1::2] = words >> 4
        vals = E2M1[nib]
    vals = vals * np.repeat(np.exp2(scales.astype(np.float64) - 127.0), 8, axis=1)[..., None]
    return vals.transpose(0, 1, 3, 2).reshape(g * 512, n)
def pack4(w):
    words, scales = pack_weight(w, "e2m1")
    return words.reshape(words.shape[0], 128, -1), scales


def unpack4(words, scales):
    return unpack_weight(words.reshape(words.shape[0], 128, -1, 2), scales, "e2m1")


T, C, E, F, D = 1024, 512, 2048, 1024, 512


def setup_inputs():
    s, r, u = mx_kscale(C), mx_kscale(E), mx_kscale(F)
    w_enc = np.random.standard_normal((E, F)) / np.sqrt(E) / r[:, None] * u
    w_key = np.random.standard_normal((F, D)) / np.sqrt(F) / u[:, None]
    w_val = np.random.standard_normal((F, D)) / np.sqrt(F) / u[:, None]
    enc_words, enc_scales = pack4(w_enc)
    key_words, key_scales = pack4(w_key)
    val_words, val_scales = pack4(w_val)
    return {"clip": bf(np.random.standard_normal((T, C)) * s),
            "enc": bf(np.random.standard_normal((T, E)) * r),
            "w_clip": bf(np.random.standard_normal((C, F)) / np.sqrt(C) / s[:, None] * u),
            "enc_words": enc_words, "enc_scales": enc_scales,
            "bias": bf(0.3 * np.random.standard_normal(F) * u),
            "key_words": key_words, "key_scales": key_scales,
            "val_words": val_words, "val_scales": val_scales,
            "emphasis": bf(np.random.uniform(0.6, 1.5, T))}


def reference(clip, enc, w_clip, enc_words, enc_scales, bias, key_words, key_scales, val_words, val_scales, emphasis):
    from_clip = mxq(f64(clip), 1, "e4m3") @ mxq(f64(w_clip), 0, "e4m3")
    from_enc = mxq(f64(enc), 1, "e4m3") @ unpack4(enc_words, enc_scales)
    context = np.maximum(from_clip + from_enc + f64(bias), 0.0)
    cq = mxq(context, 1, "e4m3")
    keys = cq @ unpack4(key_words, key_scales)
    values = (cq @ unpack4(val_words, val_scales)) * f64(emphasis)[:, None]
    return keys, values

@@ -1,0 +1,350 @@
+from contextlib import ExitStack
+
+import concourse.mybir as mybir
+from concourse.masks import make_identity
+
+T, C, E, F, D = 1024, 512, 2048, 1024, 512
+FLOPS = 2 * T * F * (C + E) + 2 * 2 * T * F * D
+
+F32 = mybir.dt.float32
+BF16 = mybir.dt.bfloat16
+I32 = mybir.dt.int32
+U32 = mybir.dt.uint32
+U8 = mybir.dt.uint8
+FP8X4 = mybir.dt.float8_e4m3fn_x4
+FP4X4 = mybir.dt.float4_e2m1fn_x4
+ACT = mybir.ActivationFunctionType
+ALU = mybir.AluOpType
+
+P = 128
+TILES = T // P
+KP = 512
+BANK = 512
+
+
+def tile_text_image_bridge_s3_kernel(
+    tc, clip, enc, w_clip, enc_words, enc_scales, bias, key_words, key_scales,
+    val_words, val_scales, emphasis, out_0, out_1,
+):
+    nc = tc.nc
+    enc_t = enc.rearrange("(p i) k -> p i k", i=TILES)
+    clip_t = clip.rearrange("(p i) k -> p (i k)", i=TILES)
+    outs = [o.rearrange("(p i) d -> p i d", i=TILES) for o in (out_0, out_1)]
+
+    with ExitStack() as ctx:
+        keep = ctx.enter_context(tc.tile_pool(name="keep", bufs=1))
+        work = ctx.enter_context(tc.tile_pool(name="work", bufs=3))
+        psum = ctx.enter_context(tc.psum_pool(name="psum", bufs=1))
+        ctx.enter_context(tc.manual_schedule())
+
+        def bank(b):
+            return psum.tile([P, BANK], F32, name="bank%d" % b, tag="bank%d" % b)
+
+        ident = keep.tile([P, P], F32, name="ident")
+        make_identity(nc, ident[:])
+        enc_plane = keep.tile([P, 4, F], U8, name="enc_plane", align_bytes=64)
+        nc.vector.memset(enc_plane[:].bitcast(I32), 0)
+        kv_plane = keep.tile([P, 2, 2, D], U8, name="kv_plane", align_bytes=64)
+        nc.vector.memset(kv_plane[:].bitcast(I32), 0)
+
+        bias_raw = keep.tile([P, 2, 4], BF16, name="bias_raw")
+        nc.scalar.dma_start(out=bias_raw[:], in_=bias.rearrange("(g j t) -> j g t", g=2, t=4))
+        emph_raw = keep.tile([P, TILES], BF16, name="emph_raw")
+        nc.scalar.dma_start(out=emph_raw[:], in_=emphasis.rearrange("(p i) -> p i", i=TILES))
+
+        raw = {}
+
+        def load_enc(i, parts):
+            width = E // parts
+            for a in range(parts):
+                t = keep.tile([P, width], BF16, name="enc_raw%d_%d" % (i, a))
+                nc.sync.dma_start(out=t[:], in_=enc_t[:, i, a * width:(a + 1) * width])
+                raw[("enc", i, a)] = t
+
+        def load_clip(m):
+            t = keep.tile([P, 2 * C], BF16, name="clip_raw%d" % m)
+            nc.sync.dma_start(out=t[:], in_=clip_t[:, 2 * m * C:2 * (m + 1) * C])
+            raw[("clip", m)] = t
+
+        def load_plane(plane, scales):
+            for q in range(4):
+                nc.sync.dma_start(
+                    out=plane[32 * q:32 * q + 4].bitcast(I32),
+                    in_=scales[:, 4 * q:4 * q + 4, :].rearrange("g r n -> r g n").bitcast(I32),
+                )
+
+        load_enc(0, 2)
+        load_plane(enc_plane, enc_scales)
+        enc_w = []
+        for g in range(4):
+            t = keep.tile([P, 2 * F], U8, name="enc_w%d" % g, align_bytes=64)
+            nc.sync.dma_start(out=t[:].bitcast(I32), in_=enc_words[g].bitcast(I32))
+            enc_w.append(t)
+        load_enc(1, 1)
+        load_clip(0)
+        wc_raw = []
+        wc_src = w_clip.rearrange("(p j) n -> p j n", j=4)
+        for h in range(2):
+            t = keep.tile([P, 4, BANK], BF16, name="wc_raw%d" % h)
+            nc.sync.dma_start(out=t[:], in_=wc_src[:, :, h * BANK:(h + 1) * BANK])
+            wc_raw.append(t)
+        load_enc(2, 1)
+        load_clip(1)
+        load_enc(3, 1)
+        kv_w = []
+        for m, words in enumerate((key_words, val_words)):
+            t = keep.tile([P, 2, 2 * D], U8, name="kv_w%d" % m, align_bytes=64)
+            nc.sync.dma_start(out=t[:].bitcast(I32), in_=words.rearrange("g p b -> p g b").bitcast(I32))
+            kv_w.append(t)
+        load_plane(kv_plane[:, 0], key_scales)
+        load_plane(kv_plane[:, 1], val_scales)
+        for i in range(4, TILES):
+            load_enc(i, 1)
+            if i % 2 == 0:
+                load_clip(i // 2)
+
+        bias_col = keep.tile([P, 8], F32, name="bias_col")
+        nc.scalar.activation(out=bias_col[:], in_=bias_raw[:].rearrange("p g t -> p (g t)"), func=ACT.Copy)
+        emph = keep.tile([P, TILES], F32, name="emph")
+        nc.scalar.activation(out=emph[:], in_=emph_raw[:], func=ACT.Copy)
+        bias_rows = keep.tile([P, 2, BANK], F32, name="bias_rows")
+
+        srt = {}
+        banks = {}
+        grouped = {}
+        quant = {}
+        acc = {}
+        ctxs = {}
+
+        def sort_words(key, src, tag):
+            words = src.shape[1] // 2
+            t = work.tile([P, 2, words // 2], F32, name=tag, tag=tag)
+            nc.vector.tensor_copy(
+                out=t[:].rearrange("p u (j i) -> p j u i", i=4),
+                in_=src[:].bitcast(F32).rearrange("p (j i u) -> p j u i", i=4, u=2),
+            )
+            srt[key] = t
+
+        def turn(key, b, pieces):
+            t = bank(b)
+            for u in range(2):
+                for c in range(2):
+                    col = (2 * u + c) * P
+                    nc.tensor.transpose(t[:, col:col + P], pieces(u, c), ident[:])
+            banks[key] = t
+
+        def turn_enc(i, a, b):
+            if ("enc", i, a) in srt:
+                s, off = srt[("enc", i, a)], 0
+            else:
+                s, off = srt[("enc", i, 0)], 2 * a
+            turn(("enc", i, a), b, lambda u, c: s[:, u, (off + c) * P:(off + c + 1) * P])
+
+        def turn_clip(m, b):
+            s = srt[("clip", m)]
+            turn(("clip", m), b, lambda u, c: s[:, u, c * P:(c + 1) * P])
+
+        def empty(key):
+            t = work.tile([P, 1024], BF16, name="grouped", tag="grouped", bufs=6, align_bytes=64)
+            nc.scalar.copy(
+                out=t[:].bitcast(F32).rearrange("p (c u) -> p c u", u=2),
+                in_=banks[key][:].rearrange("p (u c) -> p c u", u=2),
+            )
+            grouped[key] = t
+
+        def quantize(key):
+            src = grouped[key]
+            cols = src.shape[1] // 4
+            name = "_".join([str(x) for x in key])
+            codes = keep.tile([P, cols], U32, name="codes_" + name, align_bytes=64)
+            scales = keep.tile([P, cols], U8, name="scales_" + name, align_bytes=64)
+            nc.vector.quantize_mx(out=codes[:].bitcast(FP8X4), scales=scales[:], in_=src[:])
+            quant[key] = (codes, scales)
+
+        def mx(out, key, c, rhs, rhs_scale, start, stop):
+            codes, scales = quant[key]
+            nc.tensor.matmul_mx(
+                out=out[:], lhsT=codes[:, c * P:(c + 1) * P].bitcast(FP8X4),
+                lhsT_scale=scales[:, c * P:(c + 1) * P],
+                rhs=rhs, rhs_scale=rhs_scale, start=start, stop=stop,
+            )
+
+        def enc_pass(i, h, g):
+            mx(acc[(i, h)], ("enc", i, g // 2), g % 2,
+               enc_w[g][:, 2 * h * BANK:2 * (h + 1) * BANK].bitcast(FP4X4),
+               enc_plane[:, g, h * BANK:(h + 1) * BANK], g == 0, False)
+
+        def clip_pass(i, h):
+            codes, scales = quant[("wc", h)]
+            mx(acc[(i, h)], ("clip", i // 2), i % 2, codes[:].bitcast(FP8X4), scales[:], False, True)
+
+        def stage1(i, h, b):
+            acc[(i, h)] = bank(b)
+            for g in range(4):
+                enc_pass(i, h, g)
+            clip_pass(i, h)
+
+        def add_bias(i, h):
+            if h == 0:
+                ctxs[i] = work.tile([P, F], BF16, name="ctx", tag="ctx")
+            nc.vector.tensor_tensor(
+                out=ctxs[i][:, h * BANK:(h + 1) * BANK].rearrange("p (u j e) -> p u j e", u=2, e=2),
+                in0=acc[(i, h)][:].rearrange("p (j u e) -> p u j e", u=2, e=2),
+                in1=bias_rows[:, h, :].rearrange("p (u j e) -> p u j e", u=2, e=2),
+                op=ALU.add,
+            )
+
+        def turn_ctx(i, b):
+            w = ctxs[i][:].bitcast(F32)
+            turn(("ctx", i), b, lambda u, c: w[:, (2 * c + u) * P:(2 * c + u + 1) * P])
+
+        def relu(i):
+            t = work.tile([P, 1024], BF16, name="grouped", tag="grouped", bufs=6, align_bytes=64)
+            nc.scalar.activation(
+                out=t[:].rearrange("p (c u e) -> p c u e", u=2, e=2),
+                in_=banks[("ctx", i)][:].bitcast(BF16).rearrange("p (u c e) -> p c u e", u=2, e=2),
+                func=ACT.Relu,
+            )
+            grouped[("ctx", i)] = t
+
+        def stage2(i, m, b):
+            t = bank(b)
+            for g in range(2):
+                mx(t, ("ctx", i), g, kv_w[m][:, g, :].bitcast(FP4X4), kv_plane[:, m, g, :], g == 0, g == 1)
+            acc[("out", i, m)] = t
+
+        def store(i, m, on_vector=False):
+            t = work.tile([P, D], F32, name="res", tag="res", bufs=8)
+            src = acc[("out", i, m)]
+            if m == 0:
+                nc.scalar.copy(out=t[:], in_=src[:])
+            elif on_vector:
+                nc.vector.tensor_scalar(out=t[:], in0=src[:], scalar1=emph[:, i:i + 1], scalar2=None, op0=ALU.mult)
+            else:
+                nc.scalar.activation(out=t[:], in_=src[:], func=ACT.Copy, scale=emph[:, i:i + 1])
+            nc.sync.dma_start(out=outs[m][:, i, :], in_=t[:])
+
+        def interleave_wc(h, engine_copy):
+            t = keep.tile([P, 4 * BANK], BF16, name="wc_grouped%d" % h, align_bytes=64)
+            engine_copy(
+                out=t[:].rearrange("p (c i t) -> p c t i", i=4, t=4),
+                in_=wc_raw[h][:].rearrange("p t (c i) -> p c t i", i=4),
+            )
+            grouped[("wc", h)] = t
+
+        T0, T1, T2, TC, A0, A1, B0, B1 = range(8)
+
+        for a in range(2):
+            sort_words(("enc", 0, a), raw[("enc", 0, a)], "srt_half")
+        for a in range(2):
+            turn_enc(0, a, T0 + a)
+            empty(("enc", 0, a))
+        for g in range(2):
+            t = bank(B0 + g)
+            for s in range(4):
+                col = bias_col[:, 4 * g + s:4 * g + s + 1]
+                nc.tensor.transpose(t[:, s * P:(s + 1) * P], col.to_broadcast([P, P]), ident[:])
+            nc.scalar.copy(
+                out=bias_rows[:, g, :].rearrange("p (u j e) -> p u j e", u=2, e=2),
+                in_=t[:].rearrange("p (u e j) -> p u j e", u=2, e=2),
+            )
+        for a in range(2):
+            quantize(("enc", 0, a))
+        for h in range(2):
+            acc[(0, h)] = bank(A0 + h)
+        for g in range(2):
+            for h in range(2):
+                enc_pass(0, h, g)
+        sort_words(("enc", 1, 0), raw[("enc", 1, 0)], "srt")
+        sort_words(("clip", 0), raw[("clip", 0)], "srt_half")
+        for a in range(2):
+            turn_enc(1, a, T0 + a)
+            empty(("enc", 1, a))
+        turn_clip(0, T2)
+        empty(("clip", 0))
+        for g in range(2, 4):
+            for h in range(2):
+                enc_pass(0, h, g)
+        for a in range(2):
+            quantize(("enc", 1, a))
+        quantize(("clip", 0))
+        interleave_wc(0, nc.vector.tensor_copy)
+        interleave_wc(1, nc.scalar.copy)
+        for h in range(2):
+            acc[(1, h)] = bank(B0 + h)
+        for g in range(4):
+            for h in range(2):
+                enc_pass(1, h, g)
+        sort_words(("enc", 2, 0), raw[("enc", 2, 0)], "srt")
+        quantize(("wc", 0))
+        for a in range(2):
+            turn_enc(2, a, T0 + a)
+            empty(("enc", 2, a))
+        quantize(("wc", 1))
+        sort_words(("enc", 3, 0), raw[("enc", 3, 0)], "srt")
+        sort_words(("clip", 1), raw[("clip", 1)], "srt_half")
+        for i in range(2):
+            for h in range(2):
+                clip_pass(i, h)
+        turn_clip(1, T2)
+        empty(("clip", 1))
+        add_bias(0, 0)
+        quantize(("enc", 2, 0))
+        add_bias(0, 1)
+        quantize(("enc", 2, 1))
+        quantize(("clip", 1))
+        add_bias(1, 0)
+        add_bias(1, 1)
+
+        for n in range(2, TILES - 1):
+            turn_ctx(n - 2, TC)
+            relu(n - 2)
+            if n + 2 < TILES:
+                sort_words(("enc", n + 2, 0), raw[("enc", n + 2, 0)], "srt")
+                if n % 2 == 0:
+                    sort_words(("clip", n // 2 + 1), raw[("clip", n // 2 + 1)], "srt_half")
+            for a in range(2):
+                turn_enc(n + 1, a, T0 + a)
+                empty(("enc", n + 1, a))
+            if n % 2 == 1:
+                turn_clip((n + 1) // 2, T2)
+                empty(("clip", (n + 1) // 2))
+            quantize(("ctx", n - 2))
+            stage1(n, 0, A0)
+            quantize(("enc", n + 1, 0))
+            add_bias(n, 0)
+            quantize(("enc", n + 1, 1))
+            if n % 2 == 1:
+                quantize(("clip", (n + 1) // 2))
+            stage1(n, 1, A1)
+            add_bias(n, 1)
+            for m in range(2):
+                stage2(n - 2, m, B0 + m)
+                store(n - 2, m)
+
+        n = TILES - 1
+        turn_ctx(n - 2, TC)
+        relu(n - 2)
+        turn_ctx(n - 1, T0)
+        relu(n - 1)
+        quantize(("ctx", n - 2))
+        stage1(n, 0, A0)
+        quantize(("ctx", n - 1))
+        add_bias(n, 0)
+        stage1(n, 1, A1)
+        add_bias(n, 1)
+        for m in range(2):
+            stage2(n - 2, m, B0 + m)
+        store(n - 2, 0)
+        turn_ctx(n, TC)
+        relu(n)
+        store(n - 2, 1, True)
+        for m in range(2):
+            stage2(n - 1, m, T1 + m)
+        quantize(("ctx", n))
+        store(n - 1, 0)
+        store(n - 1, 1, True)
+        for m in range(2):
+            stage2(n, m, A0 + m)
+        store(n, 0)
+        store(n, 1, True)

@@ -40,26 +40,30 @@ def tile_text_image_bridge_s3_kernel(
         def bank(b):
             return psum.tile([P, BANK], F32, name="bank%d" % b, tag="bank%d" % b)
 
-        ident = keep.tile([P, P], F32, name="ident")
-        make_identity(nc, ident[:])
         enc_plane = keep.tile([P, 4, F], U8, name="enc_plane", align_bytes=64)
         nc.vector.memset(enc_plane[:].bitcast(I32), 0)
         kv_plane = keep.tile([P, 2, 2, D], U8, name="kv_plane", align_bytes=64)
         nc.vector.memset(kv_plane[:].bitcast(I32), 0)
 
         bias_raw = keep.tile([P, 2, 4], BF16, name="bias_raw")
-        nc.scalar.dma_start(out=bias_raw[:], in_=bias.rearrange("(g j t) -> j g t", g=2, t=4))
+        nc.gpsimd.dma_start(out=bias_raw[:], in_=bias.rearrange("(g j t) -> j g t", g=2, t=4))
         emph_raw = keep.tile([P, TILES], BF16, name="emph_raw")
-        nc.scalar.dma_start(out=emph_raw[:], in_=emphasis.rearrange("(p i) -> p i", i=TILES))
+        nc.gpsimd.dma_start(out=emph_raw[:], in_=emphasis.rearrange("(p i) -> p i", i=TILES))
+        ident = keep.tile([P, P], F32, name="ident")
+        make_identity(nc, ident[:])
 
         raw = {}
 
-        def load_enc(i, parts):
+        def load_enc(i, a, parts):
             width = E // parts
-            for a in range(parts):
-                t = keep.tile([P, width], BF16, name="enc_raw%d_%d" % (i, a))
-                nc.sync.dma_start(out=t[:], in_=enc_t[:, i, a * width:(a + 1) * width])
-                raw[("enc", i, a)] = t
+            t = keep.tile([P, width], BF16, name="enc_raw%d_%d" % (i, a))
+            nc.sync.dma_start(out=t[:], in_=enc_t[:, i, a * width:(a + 1) * width])
+            raw[("enc", i, a)] = t
+
+        def load_enc_w(g):
+            t = keep.tile([P, 2 * F], U8, name="enc_w%d" % g, align_bytes=64)
+            nc.sync.dma_start(out=t[:].bitcast(I32), in_=enc_words[g].bitcast(I32))
+            enc_w.append(t)
 
         def load_clip(m):
             t = keep.tile([P, 2 * C], BF16, name="clip_raw%d" % m)
@@ -73,24 +77,28 @@ def tile_text_image_bridge_s3_kernel(
                     in_=scales[:, 4 * q:4 * q + 4, :].rearrange("g r n -> r g n").bitcast(I32),
                 )
 
-        load_enc(0, 2)
-        load_plane(enc_plane, enc_scales)
         enc_w = []
-        for g in range(4):
-            t = keep.tile([P, 2 * F], U8, name="enc_w%d" % g, align_bytes=64)
-            nc.sync.dma_start(out=t[:].bitcast(I32), in_=enc_words[g].bitcast(I32))
-            enc_w.append(t)
-        load_enc(1, 1)
+        load_enc(0, 0, 2)
+        load_enc(1, 0, 2)
+        load_plane(enc_plane, enc_scales)
+        load_enc_w(0)
+        load_enc_w(1)
+        load_enc(2, 0, 2)
+        for i in range(3):
+            load_enc(i, 1, 2)
+        load_enc_w(2)
+        load_enc_w(3)
         load_clip(0)
+        load_clip(1)
         wc_raw = []
         wc_src = w_clip.rearrange("(p j) n -> p j n", j=4)
         for h in range(2):
             t = keep.tile([P, 4, BANK], BF16, name="wc_raw%d" % h)
             nc.sync.dma_start(out=t[:], in_=wc_src[:, :, h * BANK:(h + 1) * BANK])
             wc_raw.append(t)
-        load_enc(2, 1)
-        load_clip(1)
-        load_enc(3, 1)
+        load_enc(3, 0, 1)
+        load_enc(4, 0, 1)
+        load_clip(2)
         kv_w = []
         for m, words in enumerate((key_words, val_words)):
             t = keep.tile([P, 2, 2 * D], U8, name="kv_w%d" % m, align_bytes=64)
@@ -98,15 +106,14 @@ def tile_text_image_bridge_s3_kernel(
             kv_w.append(t)
         load_plane(kv_plane[:, 0], key_scales)
         load_plane(kv_plane[:, 1], val_scales)
-        for i in range(4, TILES):
-            load_enc(i, 1)
+        for i in range(5, TILES):
+            load_enc(i, 0, 1)
             if i % 2 == 0:
                 load_clip(i // 2)
 
         bias_col = keep.tile([P, 8], F32, name="bias_col")
-        nc.scalar.activation(out=bias_col[:], in_=bias_raw[:].rearrange("p g t -> p (g t)"), func=ACT.Copy)
+        nc.gpsimd.tensor_copy(out=bias_col[:], in_=bias_raw[:].rearrange("p g t -> p (g t)"))
         emph = keep.tile([P, TILES], F32, name="emph")
-        nc.scalar.activation(out=emph[:], in_=emph_raw[:], func=ACT.Copy)
         bias_rows = keep.tile([P, 2, BANK], F32, name="bias_rows")
 
         srt = {}
@@ -118,7 +125,7 @@ def tile_text_image_bridge_s3_kernel(
 
         def sort_words(key, src, tag):
             words = src.shape[1] // 2
-            t = work.tile([P, 2, words // 2], F32, name=tag, tag=tag)
+            t = work.tile([P, 2, words // 2], F32, name=tag, tag=tag, bufs=4)
             nc.vector.tensor_copy(
                 out=t[:].rearrange("p u (j i) -> p j u i", i=4),
                 in_=src[:].bitcast(F32).rearrange("p (j i u) -> p j u i", i=4, u=2),
@@ -186,7 +193,7 @@ def tile_text_image_bridge_s3_kernel(
 
         def add_bias(i, h):
             if h == 0:
-                ctxs[i] = work.tile([P, F], BF16, name="ctx", tag="ctx")
+                ctxs[i] = work.tile([P, F], BF16, name="ctx", tag="ctx", bufs=4)
             nc.vector.tensor_tensor(
                 out=ctxs[i][:, h * BANK:(h + 1) * BANK].rearrange("p (u j e) -> p u j e", u=2, e=2),
                 in0=acc[(i, h)][:].rearrange("p (j u e) -> p u j e", u=2, e=2),
@@ -234,11 +241,27 @@ def tile_text_image_bridge_s3_kernel(
 
         T0, T1, T2, TC, A0, A1, B0, B1 = range(8)
 
-        for a in range(2):
-            sort_words(("enc", 0, a), raw[("enc", 0, a)], "srt_half")
-        for a in range(2):
-            turn_enc(0, a, T0 + a)
-            empty(("enc", 0, a))
+        head_banks = [(T2, TC), (A0, A1), (B0, B1)]
+
+        def sort_half(i, a):
+            sort_words(("enc", i, a), raw[("enc", i, a)], "srt_half")
+
+        def turn_pair(first, second):
+            for b, (i, a) in enumerate((first, second)):
+                turn_enc(i, a, T0 + b)
+                empty(("enc", i, a))
+
+        def head_passes(i, a):
+            if a == 0:
+                for h in range(2):
+                    acc[(i, h)] = bank(head_banks[i][h])
+            for g in range(2 * a, 2 * a + 2):
+                for h in range(2):
+                    enc_pass(i, h, g)
+
+        sort_half(0, 0)
+        sort_half(1, 0)
+        turn_pair((0, 0), (1, 0))
         for g in range(2):
             t = bank(B0 + g)
             for s in range(4):
@@ -248,85 +271,97 @@ def tile_text_image_bridge_s3_kernel(
                 out=bias_rows[:, g, :].rearrange("p (u j e) -> p u j e", u=2, e=2),
                 in_=t[:].rearrange("p (u e j) -> p u j e", u=2, e=2),
             )
-        for a in range(2):
-            quantize(("enc", 0, a))
-        for h in range(2):
-            acc[(0, h)] = bank(A0 + h)
-        for g in range(2):
-            for h in range(2):
-                enc_pass(0, h, g)
-        sort_words(("enc", 1, 0), raw[("enc", 1, 0)], "srt")
-        sort_words(("clip", 0), raw[("clip", 0)], "srt_half")
-        for a in range(2):
-            turn_enc(1, a, T0 + a)
-            empty(("enc", 1, a))
-        turn_clip(0, T2)
-        empty(("clip", 0))
-        for g in range(2, 4):
-            for h in range(2):
-                enc_pass(0, h, g)
-        for a in range(2):
-            quantize(("enc", 1, a))
-        quantize(("clip", 0))
-        interleave_wc(0, nc.vector.tensor_copy)
-        interleave_wc(1, nc.scalar.copy)
-        for h in range(2):
-            acc[(1, h)] = bank(B0 + h)
-        for g in range(4):
-            for h in range(2):
-                enc_pass(1, h, g)
-        sort_words(("enc", 2, 0), raw[("enc", 2, 0)], "srt")
-        quantize(("wc", 0))
-        for a in range(2):
-            turn_enc(2, a, T0 + a)
-            empty(("enc", 2, a))
-        quantize(("wc", 1))
+        nc.scalar.activation(out=emph[:], in_=emph_raw[:], func=ACT.Copy)
+        quantize(("enc", 0, 0))
+        quantize(("enc", 1, 0))
+        head_passes(0, 0)
+        sort_half(2, 0)
+        sort_half(0, 1)
+        turn_pair((2, 0), (0, 1))
+        head_passes(1, 0)
+        sort_half(1, 1)
+        sort_half(2, 1)
+        quantize(("enc", 2, 0))
+        quantize(("enc", 0, 1))
+        turn_pair((1, 1), (2, 1))
+        head_passes(2, 0)
+        head_passes(0, 1)
+        for m in range(2):
+            sort_words(("clip", m), raw[("clip", m)], "srt_half")
+        quantize(("enc", 1, 1))
+        quantize(("enc", 2, 1))
+        interleave_wc(0, nc.scalar.copy)
+        for m in range(2):
+            turn_clip(m, T0 + m)
+            empty(("clip", m))
+        head_passes(1, 1)
+        head_passes(2, 1)
+        interleave_wc(1, nc.vector.tensor_copy)
         sort_words(("enc", 3, 0), raw[("enc", 3, 0)], "srt")
-        sort_words(("clip", 1), raw[("clip", 1)], "srt_half")
-        for i in range(2):
+        quantize(("wc", 0))
+        quantize(("clip", 0))
+        turn_pair((3, 0), (3, 1))
+        quantize(("wc", 1))
+        quantize(("clip", 1))
+        for i in (1, 0, 2):
             for h in range(2):
                 clip_pass(i, h)
-        turn_clip(1, T2)
-        empty(("clip", 1))
-        add_bias(0, 0)
-        quantize(("enc", 2, 0))
-        add_bias(0, 1)
-        quantize(("enc", 2, 1))
-        quantize(("clip", 1))
         add_bias(1, 0)
+        quantize(("enc", 3, 0))
+        quantize(("enc", 3, 1))
+        sort_words(("enc", 4, 0), raw[("enc", 4, 0)], "srt")
+        add_bias(0, 0)
+        add_bias(0, 1)
+        sort_words(("clip", 2), raw[("clip", 2)], "srt_half")
         add_bias(1, 1)
+        stage1(3, 0, A0)
+        add_bias(2, 0)
+        add_bias(2, 1)
 
-        for n in range(2, TILES - 1):
-            turn_ctx(n - 2, TC)
-            relu(n - 2)
+        LAG = 3
+        for n in range(LAG, TILES - 1):
+            turn_enc(n + 1, 0, T0)
+            empty(("enc", n + 1, 0))
+            turn_ctx(n - LAG, TC)
+            relu(n - LAG)
+            turn_enc(n + 1, 1, T1)
+            empty(("enc", n + 1, 1))
+            if n % 2 == 1:
+                turn_clip((n + 1) // 2, T2)
+                empty(("clip", (n + 1) // 2))
+            if n == TILES - 2:
+                turn_ctx(n - LAG + 1, T2)
+                relu(n - LAG + 1)
+            if n == LAG:
+                quantize(("ctx", n - LAG))
             if n + 2 < TILES:
                 sort_words(("enc", n + 2, 0), raw[("enc", n + 2, 0)], "srt")
                 if n % 2 == 0:
                     sort_words(("clip", n // 2 + 1), raw[("clip", n // 2 + 1)], "srt_half")
-            for a in range(2):
-                turn_enc(n + 1, a, T0 + a)
-                empty(("enc", n + 1, a))
-            if n % 2 == 1:
-                turn_clip((n + 1) // 2, T2)
-                empty(("clip", (n + 1) // 2))
-            quantize(("ctx", n - 2))
-            stage1(n, 0, A0)
             quantize(("enc", n + 1, 0))
+            if n > LAG:
+                stage1(n, 0, A0)
+                quantize(("ctx", n - LAG))
             add_bias(n, 0)
             quantize(("enc", n + 1, 1))
             if n % 2 == 1:
                 quantize(("clip", (n + 1) // 2))
+            if n == TILES - 2:
+                quantize(("ctx", n - LAG + 1))
             stage1(n, 1, A1)
             add_bias(n, 1)
             for m in range(2):
-                stage2(n - 2, m, B0 + m)
-                store(n - 2, m)
+                stage2(n - LAG, m, B0 + m)
+                store(n - LAG, m)
 
         n = TILES - 1
         turn_ctx(n - 2, TC)
         relu(n - 2)
         turn_ctx(n - 1, T0)
         relu(n - 1)
+        for m in range(2):
+            stage2(n - 3, m, B0 + m)
+            store(n - 3, m)
         quantize(("ctx", n - 2))
         stage1(n, 0, A0)
         quantize(("ctx", n - 1))
@@ -336,15 +371,29 @@ def tile_text_image_bridge_s3_kernel(
         for m in range(2):
             stage2(n - 2, m, B0 + m)
         store(n - 2, 0)
-        turn_ctx(n, TC)
-        relu(n)
         store(n - 2, 1, True)
+        w = ctxs[n][:].bitcast(F32)
+        for h in range(2):
+            t = bank(T1 + h)
+            for u in range(2):
+                nc.tensor.transpose(t[:, u * P:(u + 1) * P], w[:, (2 * h + u) * P:(2 * h + u + 1) * P], ident[:])
+            half = keep.tile([P, 512], BF16, name="last%d" % h, align_bytes=64)
+            dst = half[:].rearrange("p (c u e) -> p c u e", u=2, e=2)
+            src = t[:, 0:2 * P].bitcast(BF16).rearrange("p (u c e) -> p c u e", u=2, e=2)
+            if h == 0:
+                nc.scalar.activation(out=dst, in_=src, func=ACT.Relu)
+            else:
+                nc.vector.tensor_scalar(out=dst, in0=src, scalar1=0.0, scalar2=None, op0=ALU.max)
+            grouped[("last", h)] = half
         for m in range(2):
-            stage2(n - 1, m, T1 + m)
-        quantize(("ctx", n))
+            stage2(n - 1, m, (TC, T0)[m])
+        quantize(("last", 0))
+        quantize(("last", 1))
         store(n - 1, 0)
         store(n - 1, 1, True)
         for m in range(2):
-            stage2(n, m, A0 + m)
+            acc[("out", n, m)] = bank(A0 + m)
+            for g in range(2):
+                mx(acc[("out", n, m)], ("last", g), 0, kv_w[m][:, g, :].bitcast(FP4X4), kv_plane[:, m, g, :], g == 0, g == 1)
         store(n, 0)
         store(n, 1, True)

@@ -20,6 +20,7 @@ P = 128
 TILES = T // P
 KP = 512
 BANK = 512
+VP = 6
 
 
 def tile_text_image_bridge_s3_kernel(
@@ -40,18 +41,20 @@ def tile_text_image_bridge_s3_kernel(
         def bank(b):
             return psum.tile([P, BANK], F32, name="bank%d" % b, tag="bank%d" % b)
 
-        enc_plane = keep.tile([P, 4, F], U8, name="enc_plane", align_bytes=64)
-        nc.vector.memset(enc_plane[:].bitcast(I32), 0)
+        enc_planes = []
+        for a in range(2):
+            t = keep.tile([P, 2, F], U8, name="enc_plane%d" % a, align_bytes=64)
+            nc.vector.memset(t[:].bitcast(I32), 0)
+            enc_planes.append(t)
         kv_plane = keep.tile([P, 2, 2, D], U8, name="kv_plane", align_bytes=64)
         nc.vector.memset(kv_plane[:].bitcast(I32), 0)
 
+        ident = keep.tile([P, P], F32, name="ident")
+        make_identity(nc, ident[:])
         bias_raw = keep.tile([P, 2, 4], BF16, name="bias_raw")
         nc.gpsimd.dma_start(out=bias_raw[:], in_=bias.rearrange("(g j t) -> j g t", g=2, t=4))
         emph_raw = keep.tile([P, TILES], BF16, name="emph_raw")
         nc.gpsimd.dma_start(out=emph_raw[:], in_=emphasis.rearrange("(p i) -> p i", i=TILES))
-        ident = keep.tile([P, P], F32, name="ident")
-        make_identity(nc, ident[:])
-
         raw = {}
 
         def load_enc(i, a, parts):
@@ -80,12 +83,13 @@ def tile_text_image_bridge_s3_kernel(
         enc_w = []
         load_enc(0, 0, 2)
         load_enc(1, 0, 2)
-        load_plane(enc_plane, enc_scales)
+        load_plane(enc_planes[0], enc_scales[0:2])
         load_enc_w(0)
         load_enc_w(1)
         load_enc(2, 0, 2)
         for i in range(3):
             load_enc(i, 1, 2)
+        load_plane(enc_planes[1], enc_scales[2:4])
         load_enc_w(2)
         load_enc_w(3)
         load_clip(0)
@@ -106,10 +110,15 @@ def tile_text_image_bridge_s3_kernel(
             kv_w.append(t)
         load_plane(kv_plane[:, 0], key_scales)
         load_plane(kv_plane[:, 1], val_scales)
-        for i in range(5, TILES):
+        for i in range(5, VP):
             load_enc(i, 0, 1)
-            if i % 2 == 0:
-                load_clip(i // 2)
+        late = TILES - VP
+        late_raw = keep.tile([P, 4, late * 4, P], BF16, name="late_raw")
+        late_src = enc.rearrange("t (g y) -> (t g) y", g=4).rearrange("(s r j) (q k) -> q s r j k", s=4, j=4 * TILES, q=4)
+        for s in range(4):
+            for q in (0, 2, 1, 3):
+                nc.sync.dma_start(out=late_raw[32 * q:32 * (q + 1), s], in_=late_src[q, s, :, 4 * VP:, :])
+        load_clip(3)
 
         bias_col = keep.tile([P, 8], F32, name="bias_col")
         nc.gpsimd.tensor_copy(out=bias_col[:], in_=bias_raw[:].rearrange("p g t -> p (g t)"))
@@ -125,7 +134,7 @@ def tile_text_image_bridge_s3_kernel(
 
         def sort_words(key, src, tag):
             words = src.shape[1] // 2
-            t = work.tile([P, 2, words // 2], F32, name=tag, tag=tag, bufs=4)
+            t = work.tile([P, 2, words // 2], F32, name=tag, tag=tag, bufs=4, align_bytes=64)
             nc.vector.tensor_copy(
                 out=t[:].rearrange("p u (j i) -> p j u i", i=4),
                 in_=src[:].bitcast(F32).rearrange("p (j i u) -> p j u i", i=4, u=2),
@@ -150,6 +159,22 @@ def tile_text_image_bridge_s3_kernel(
         def turn_clip(m, b):
             s = srt[("clip", m)]
             turn(("clip", m), b, lambda u, c: s[:, u, c * P:(c + 1) * P])
+
+        def sort_late(i, a):
+            t = work.tile([P, 2, 2, 4, 32], F32, name="srt_half", tag="srt_half", bufs=4, align_bytes=64)
+            first = 4 * (i - VP) + 2 * a
+            src = late_raw[:, :, first:first + 2, :].bitcast(F32)
+            nc.vector.tensor_copy(
+                out=t[:].rearrange("p u c s j -> p s c u j"),
+                in_=src.rearrange("p s c (j u) -> p s c u j", u=2),
+            )
+            srt[("enc", i, a)] = t
+
+        def turn_late(i, a):
+            t = work.tile([P, BANK], F32, name="turned", tag="turned", align_bytes=64)
+            nc.vector.transpose(t[:], srt[("enc", i, a)][:].rearrange("p u c s j -> p (u c s j)"))
+            banks[("enc", i, a)] = t
+            empty(("enc", i, a))
 
         def empty(key):
             t = work.tile([P, 1024], BF16, name="grouped", tag="grouped", bufs=6, align_bytes=64)
@@ -179,7 +204,7 @@ def tile_text_image_bridge_s3_kernel(
         def enc_pass(i, h, g):
             mx(acc[(i, h)], ("enc", i, g // 2), g % 2,
                enc_w[g][:, 2 * h * BANK:2 * (h + 1) * BANK].bitcast(FP4X4),
-               enc_plane[:, g, h * BANK:(h + 1) * BANK], g == 0, False)
+               enc_planes[g // 2][:, g % 2, h * BANK:(h + 1) * BANK], g == 0, False)
 
         def clip_pass(i, h):
             codes, scales = quant[("wc", h)]
@@ -319,40 +344,72 @@ def tile_text_image_bridge_s3_kernel(
         add_bias(2, 1)
 
         LAG = 3
-        for n in range(LAG, TILES - 1):
+        for n in range(LAG, VP - 1):
             turn_enc(n + 1, 0, T0)
             empty(("enc", n + 1, 0))
             turn_ctx(n - LAG, TC)
             relu(n - LAG)
             turn_enc(n + 1, 1, T1)
             empty(("enc", n + 1, 1))
-            if n % 2 == 1:
-                turn_clip((n + 1) // 2, T2)
-                empty(("clip", (n + 1) // 2))
-            if n == TILES - 2:
-                turn_ctx(n - LAG + 1, T2)
-                relu(n - LAG + 1)
             if n == LAG:
+                turn_clip(2, T2)
+                empty(("clip", 2))
                 quantize(("ctx", n - LAG))
-            if n + 2 < TILES:
                 sort_words(("enc", n + 2, 0), raw[("enc", n + 2, 0)], "srt")
-                if n % 2 == 0:
-                    sort_words(("clip", n // 2 + 1), raw[("clip", n // 2 + 1)], "srt_half")
             quantize(("enc", n + 1, 0))
             if n > LAG:
                 stage1(n, 0, A0)
                 quantize(("ctx", n - LAG))
             add_bias(n, 0)
             quantize(("enc", n + 1, 1))
-            if n % 2 == 1:
-                quantize(("clip", (n + 1) // 2))
-            if n == TILES - 2:
-                quantize(("ctx", n - LAG + 1))
+            if n == LAG:
+                quantize(("clip", 2))
+            else:
+                sort_words(("clip", 3), raw[("clip", 3)], "srt_half")
+                sort_late(VP, 0)
+                sort_late(VP, 1)
             stage1(n, 1, A1)
             add_bias(n, 1)
             for m in range(2):
                 stage2(n - LAG, m, B0 + m)
                 store(n - LAG, m)
+
+        turn_ctx(2, TC)
+        relu(2)
+        turn_clip(3, T2)
+        turn_ctx(3, T0)
+        turn_ctx(4, T1)
+        turn_late(6, 0)
+        turn_late(6, 1)
+        empty(("clip", 3))
+        relu(3)
+        quantize(("ctx", 2))
+        stage1(5, 0, A0)
+        add_bias(5, 0)
+        quantize(("enc", 6, 0))
+        quantize(("enc", 6, 1))
+        quantize(("clip", 3))
+        sort_late(7, 0)
+        sort_late(7, 1)
+        stage1(5, 1, A1)
+        add_bias(5, 1)
+        for m in range(2):
+            stage2(2, m, B0 + m)
+            store(2, m)
+        relu(4)
+        turn_late(7, 0)
+        quantize(("ctx", 3))
+        turn_late(7, 1)
+        stage1(6, 0, A0)
+        add_bias(6, 0)
+        stage1(6, 1, A1)
+        add_bias(6, 1)
+        quantize(("ctx", 4))
+        quantize(("enc", 7, 0))
+        quantize(("enc", 7, 1))
+        for m in range(2):
+            stage2(3, m, B0 + m)
+            store(3, m)
 
         n = TILES - 1
         turn_ctx(n - 2, TC)

@@ -20,7 +20,7 @@ P = 128
 TILES = T // P
 KP = 512
 BANK = 512
-VP = 6
+VP = 4
 
 
 def tile_text_image_bridge_s3_kernel(
@@ -87,38 +87,45 @@ def tile_text_image_bridge_s3_kernel(
         load_enc_w(0)
         load_enc_w(1)
         load_enc(2, 0, 2)
-        for i in range(3):
-            load_enc(i, 1, 2)
+        wc_raw = []
+        wc_src = w_clip.rearrange("(p j) n -> p j n", j=4)
+
+        def load_wc(h):
+            t = keep.tile([P, 4, BANK], BF16, name="wc_raw%d" % h)
+            nc.sync.dma_start(out=t[:], in_=wc_src[:, :, h * BANK:(h + 1) * BANK])
+            wc_raw.append(t)
+
+        load_enc(0, 1, 2)
+        load_wc(0)
+        load_enc(1, 1, 2)
+        load_enc(2, 1, 2)
         load_plane(enc_planes[1], enc_scales[2:4])
         load_enc_w(2)
         load_enc_w(3)
         load_clip(0)
         load_clip(1)
-        wc_raw = []
-        wc_src = w_clip.rearrange("(p j) n -> p j n", j=4)
-        for h in range(2):
-            t = keep.tile([P, 4, BANK], BF16, name="wc_raw%d" % h)
-            nc.sync.dma_start(out=t[:], in_=wc_src[:, :, h * BANK:(h + 1) * BANK])
-            wc_raw.append(t)
+        load_wc(1)
         load_enc(3, 0, 1)
-        load_enc(4, 0, 1)
+        late_src = enc.rearrange("t (g y) -> (t g) y", g=4).rearrange("(s r j) (q k) -> q s r j k", s=4, j=4 * TILES, q=4)
+
+        def load_late(m):
+            t = keep.tile([P, 4, 8, P], BF16, name="late_raw%d" % m)
+            for s in range(4):
+                for q in (0, 2, 1, 3):
+                    nc.sync.dma_start(out=t[32 * q:32 * (q + 1), s], in_=late_src[q, s, :, 8 * m:8 * (m + 1), :])
+            raw[("late", m)] = t
+
         load_clip(2)
+        load_late(2)
+        load_plane(kv_plane[:, 0], key_scales)
+        load_plane(kv_plane[:, 1], val_scales)
         kv_w = []
         for m, words in enumerate((key_words, val_words)):
             t = keep.tile([P, 2, 2 * D], U8, name="kv_w%d" % m, align_bytes=64)
             nc.sync.dma_start(out=t[:].bitcast(I32), in_=words.rearrange("g p b -> p g b").bitcast(I32))
             kv_w.append(t)
-        load_plane(kv_plane[:, 0], key_scales)
-        load_plane(kv_plane[:, 1], val_scales)
-        for i in range(5, VP):
-            load_enc(i, 0, 1)
-        late = TILES - VP
-        late_raw = keep.tile([P, 4, late * 4, P], BF16, name="late_raw")
-        late_src = enc.rearrange("t (g y) -> (t g) y", g=4).rearrange("(s r j) (q k) -> q s r j k", s=4, j=4 * TILES, q=4)
-        for s in range(4):
-            for q in (0, 2, 1, 3):
-                nc.sync.dma_start(out=late_raw[32 * q:32 * (q + 1), s], in_=late_src[q, s, :, 4 * VP:, :])
         load_clip(3)
+        load_late(3)
 
         bias_col = keep.tile([P, 8], F32, name="bias_col")
         nc.gpsimd.tensor_copy(out=bias_col[:], in_=bias_raw[:].rearrange("p g t -> p (g t)"))
@@ -132,10 +139,10 @@ def tile_text_image_bridge_s3_kernel(
         acc = {}
         ctxs = {}
 
-        def sort_words(key, src, tag):
+        def sort_words(key, src, tag, engine_copy=nc.vector.tensor_copy):
             words = src.shape[1] // 2
             t = work.tile([P, 2, words // 2], F32, name=tag, tag=tag, bufs=4, align_bytes=64)
-            nc.vector.tensor_copy(
+            engine_copy(
                 out=t[:].rearrange("p u (j i) -> p j u i", i=4),
                 in_=src[:].bitcast(F32).rearrange("p (j i u) -> p j u i", i=4, u=2),
             )
@@ -160,11 +167,11 @@ def tile_text_image_bridge_s3_kernel(
             s = srt[("clip", m)]
             turn(("clip", m), b, lambda u, c: s[:, u, c * P:(c + 1) * P])
 
-        def sort_late(i, a):
+        def sort_late(i, a, engine_copy):
             t = work.tile([P, 2, 2, 4, 32], F32, name="srt_half", tag="srt_half", bufs=4, align_bytes=64)
-            first = 4 * (i - VP) + 2 * a
-            src = late_raw[:, :, first:first + 2, :].bitcast(F32)
-            nc.vector.tensor_copy(
+            first = 4 * (i % 2) + 2 * a
+            src = raw[("late", i // 2)][:, :, first:first + 2, :].bitcast(F32)
+            engine_copy(
                 out=t[:].rearrange("p u c s j -> p s c u j"),
                 in_=src.rearrange("p s c (j u) -> p s c u j", u=2),
             )
@@ -177,7 +184,7 @@ def tile_text_image_bridge_s3_kernel(
             empty(("enc", i, a))
 
         def empty(key):
-            t = work.tile([P, 1024], BF16, name="grouped", tag="grouped", bufs=6, align_bytes=64)
+            t = work.tile([P, 1024], BF16, name="grouped", tag="grouped", bufs=8, align_bytes=64)
             nc.scalar.copy(
                 out=t[:].bitcast(F32).rearrange("p (c u) -> p c u", u=2),
                 in_=banks[key][:].rearrange("p (u c) -> p c u", u=2),
@@ -218,7 +225,7 @@ def tile_text_image_bridge_s3_kernel(
 
         def add_bias(i, h):
             if h == 0:
-                ctxs[i] = work.tile([P, F], BF16, name="ctx", tag="ctx", bufs=4)
+                ctxs[i] = work.tile([P, F], BF16, name="ctx", tag="ctx", bufs=5)
             nc.vector.tensor_tensor(
                 out=ctxs[i][:, h * BANK:(h + 1) * BANK].rearrange("p (u j e) -> p u j e", u=2, e=2),
                 in0=acc[(i, h)][:].rearrange("p (j u e) -> p u j e", u=2, e=2),
@@ -231,7 +238,7 @@ def tile_text_image_bridge_s3_kernel(
             turn(("ctx", i), b, lambda u, c: w[:, (2 * c + u) * P:(2 * c + u + 1) * P])
 
         def relu(i):
-            t = work.tile([P, 1024], BF16, name="grouped", tag="grouped", bufs=6, align_bytes=64)
+            t = work.tile([P, 1024], BF16, name="grouped", tag="grouped", bufs=8, align_bytes=64)
             nc.scalar.activation(
                 out=t[:].rearrange("p (c u e) -> p c u e", u=2, e=2),
                 in_=banks[("ctx", i)][:].bitcast(BF16).rearrange("p (u c e) -> p c u e", u=2, e=2),
@@ -304,81 +311,92 @@ def tile_text_image_bridge_s3_kernel(
         sort_half(0, 1)
         turn_pair((2, 0), (0, 1))
         head_passes(1, 0)
+        interleave_wc(0, nc.vector.tensor_copy)
         sort_half(1, 1)
         sort_half(2, 1)
         quantize(("enc", 2, 0))
         quantize(("enc", 0, 1))
         turn_pair((1, 1), (2, 1))
+        quantize(("wc", 0))
         head_passes(2, 0)
         head_passes(0, 1)
-        for m in range(2):
-            sort_words(("clip", m), raw[("clip", m)], "srt_half")
+        vcopy, scopy = nc.vector.tensor_copy, nc.scalar.copy
         quantize(("enc", 1, 1))
+        sort_words(("clip", 0), raw[("clip", 0)], "srt_half")
         quantize(("enc", 2, 1))
-        interleave_wc(0, nc.scalar.copy)
+        sort_words(("clip", 1), raw[("clip", 1)], "srt_half")
         for m in range(2):
             turn_clip(m, T0 + m)
             empty(("clip", m))
         head_passes(1, 1)
-        head_passes(2, 1)
-        interleave_wc(1, nc.vector.tensor_copy)
-        sort_words(("enc", 3, 0), raw[("enc", 3, 0)], "srt")
-        quantize(("wc", 0))
+        interleave_wc(1, vcopy)
+        sort_words(("enc", 3, 0), raw[("enc", 3, 0)], "srt", scopy)
         quantize(("clip", 0))
-        turn_pair((3, 0), (3, 1))
         quantize(("wc", 1))
         quantize(("clip", 1))
-        for i in (1, 0, 2):
-            for h in range(2):
-                clip_pass(i, h)
+        for h in range(2):
+            enc_pass(2, h, 2)
+        clip_pass(0, 0)
+        clip_pass(1, 0)
+        turn_pair((3, 0), (3, 1))
+        clip_pass(0, 1)
+        clip_pass(1, 1)
+        for h in range(2):
+            enc_pass(2, h, 3)
+        clip_pass(2, 0)
+        clip_pass(2, 1)
+        add_bias(0, 0)
         add_bias(1, 0)
+        add_bias(0, 1)
         quantize(("enc", 3, 0))
         quantize(("enc", 3, 1))
-        sort_words(("enc", 4, 0), raw[("enc", 4, 0)], "srt")
-        add_bias(0, 0)
-        add_bias(0, 1)
-        sort_words(("clip", 2), raw[("clip", 2)], "srt_half")
         add_bias(1, 1)
+        sort_words(("clip", 2), raw[("clip", 2)], "srt_half", scopy)
+        sort_late(4, 0, scopy)
+        sort_late(4, 1, scopy)
         stage1(3, 0, A0)
+        turn_ctx(0, TC)
+        relu(0)
+        turn_clip(2, T2)
+        turn_ctx(1, T0)
         add_bias(2, 0)
         add_bias(2, 1)
-
-        LAG = 3
-        for n in range(LAG, VP - 1):
-            turn_enc(n + 1, 0, T0)
-            empty(("enc", n + 1, 0))
-            turn_ctx(n - LAG, TC)
-            relu(n - LAG)
-            turn_enc(n + 1, 1, T1)
-            empty(("enc", n + 1, 1))
-            if n == LAG:
-                turn_clip(2, T2)
-                empty(("clip", 2))
-                quantize(("ctx", n - LAG))
-                sort_words(("enc", n + 2, 0), raw[("enc", n + 2, 0)], "srt")
-            quantize(("enc", n + 1, 0))
-            if n > LAG:
-                stage1(n, 0, A0)
-                quantize(("ctx", n - LAG))
-            add_bias(n, 0)
-            quantize(("enc", n + 1, 1))
-            if n == LAG:
-                quantize(("clip", 2))
-            else:
-                sort_words(("clip", 3), raw[("clip", 3)], "srt_half")
-                sort_late(VP, 0)
-                sort_late(VP, 1)
-            stage1(n, 1, A1)
-            add_bias(n, 1)
-            for m in range(2):
-                stage2(n - LAG, m, B0 + m)
-                store(n - LAG, m)
-
+        turn_late(4, 0)
+        turn_late(4, 1)
+        quantize(("ctx", 0))
+        empty(("clip", 2))
+        add_bias(3, 0)
+        quantize(("enc", 4, 0))
+        quantize(("enc", 4, 1))
+        quantize(("clip", 2))
+        stage1(3, 1, A1)
+        add_bias(3, 1)
+        for m in range(2):
+            stage2(0, m, B0 + m)
+            store(0, m)
+        relu(1)
+        sort_late(5, 0, vcopy)
+        sort_late(5, 1, vcopy)
+        turn_late(5, 0)
+        quantize(("ctx", 1))
+        turn_late(5, 1)
+        sort_words(("clip", 3), raw[("clip", 3)], "srt_half")
+        stage1(4, 0, A0)
+        add_bias(4, 0)
+        stage1(4, 1, A1)
+        add_bias(4, 1)
+        quantize(("enc", 5, 0))
+        quantize(("enc", 5, 1))
+        for m in range(2):
+            stage2(1, m, B0 + m)
+            store(1, m)
         turn_ctx(2, TC)
         relu(2)
         turn_clip(3, T2)
         turn_ctx(3, T0)
         turn_ctx(4, T1)
+        sort_late(6, 0, vcopy)
+        sort_late(6, 1, vcopy)
         turn_late(6, 0)
         turn_late(6, 1)
         empty(("clip", 3))
@@ -389,14 +407,14 @@ def tile_text_image_bridge_s3_kernel(
         quantize(("enc", 6, 0))
         quantize(("enc", 6, 1))
         quantize(("clip", 3))
-        sort_late(7, 0)
-        sort_late(7, 1)
         stage1(5, 1, A1)
         add_bias(5, 1)
         for m in range(2):
             stage2(2, m, B0 + m)
             store(2, m)
         relu(4)
+        sort_late(7, 0, vcopy)
+        sort_late(7, 1, vcopy)
         turn_late(7, 0)
         quantize(("ctx", 3))
         turn_late(7, 1)

@@ -18,9 +18,14 @@ ALU = mybir.AluOpType
 
 P = 128
 TILES = T // P
-KP = 512
 BANK = 512
-VP = 4
+UNIT = 2 * BANK
+QUAD = 32
+
+TURN0, TURN1, TURN2, TURN3, CTX0, CTX1, OUT0, OUT1 = range(8)
+HEAD_BANKS = ((TURN2, TURN3), (CTX0, CTX1), (OUT0, OUT1))
+
+SORTED_BUFS, TURNED_BUFS, WOVEN_BUFS, CONTEXT_BUFS, RESULT_BUFS = 4, 3, 8, 5, 8
 
 
 def tile_text_image_bridge_s3_kernel(
@@ -28,40 +33,56 @@ def tile_text_image_bridge_s3_kernel(
     val_words, val_scales, emphasis, out_0, out_1,
 ):
     nc = tc.nc
-    enc_t = enc.rearrange("(p i) k -> p i k", i=TILES)
-    clip_t = clip.rearrange("(p i) k -> p (i k)", i=TILES)
+    vector_copy, scalar_copy = nc.vector.tensor_copy, nc.scalar.copy
+    enc_rows = enc.rearrange("(p i) k -> p i k", i=TILES)
+    enc_quads = enc.rearrange("t (g y) -> (t g) y", g=4).rearrange(
+        "(s r j) (q k) -> q s r j k", s=4, j=4 * TILES, q=4)
+    clip_rows = clip.rearrange("(p i) k -> p (i k)", i=TILES)
+    w_clip_rows = w_clip.rearrange("(p t) n -> p t n", t=4)
     outs = [o.rearrange("(p i) d -> p i d", i=TILES) for o in (out_0, out_1)]
 
-    with ExitStack() as ctx:
-        keep = ctx.enter_context(tc.tile_pool(name="keep", bufs=1))
-        work = ctx.enter_context(tc.tile_pool(name="work", bufs=3))
-        psum = ctx.enter_context(tc.psum_pool(name="psum", bufs=1))
-        ctx.enter_context(tc.manual_schedule())
+    with ExitStack() as stack:
+        keep = stack.enter_context(tc.tile_pool(name="keep", bufs=1))
+        work = stack.enter_context(tc.tile_pool(name="work", bufs=TURNED_BUFS))
+        psum = stack.enter_context(tc.psum_pool(name="psum", bufs=1))
+        stack.enter_context(tc.manual_schedule())
 
         def bank(b):
             return psum.tile([P, BANK], F32, name="bank%d" % b, tag="bank%d" % b)
 
         enc_planes = []
         for a in range(2):
-            t = keep.tile([P, 2, F], U8, name="enc_plane%d" % a, align_bytes=64)
-            nc.vector.memset(t[:].bitcast(I32), 0)
-            enc_planes.append(t)
-        kv_plane = keep.tile([P, 2, 2, D], U8, name="kv_plane", align_bytes=64)
-        nc.vector.memset(kv_plane[:].bitcast(I32), 0)
+            plane = keep.tile([P, 2, F], U8, name="enc_plane%d" % a, align_bytes=64)
+            nc.vector.memset(plane[:].bitcast(I32), 0)
+            enc_planes.append(plane)
+        val_plane = keep.tile([P, 2, D], U8, name="val_plane", align_bytes=64)
+        nc.vector.memset(val_plane[:].bitcast(I32), 0)
+        key_plane = keep.tile([P, 2, D], U8, name="key_plane", align_bytes=64)
+        out_planes = (key_plane, val_plane)
 
         ident = keep.tile([P, P], F32, name="ident")
         make_identity(nc, ident[:])
         bias_raw = keep.tile([P, 2, 4], BF16, name="bias_raw")
-        nc.gpsimd.dma_start(out=bias_raw[:], in_=bias.rearrange("(g j t) -> j g t", g=2, t=4))
+        nc.gpsimd.dma_start(out=bias_raw[:], in_=bias.rearrange("(h j t) -> j h t", h=2, t=4))
         emph_raw = keep.tile([P, TILES], BF16, name="emph_raw")
         nc.gpsimd.dma_start(out=emph_raw[:], in_=emphasis.rearrange("(p i) -> p i", i=TILES))
-        raw = {}
 
-        def load_enc(i, a, parts):
+        raw = {}
+        enc_w = []
+        out_w = []
+
+        def load_enc(i, part, parts):
             width = E // parts
-            t = keep.tile([P, width], BF16, name="enc_raw%d_%d" % (i, a))
-            nc.sync.dma_start(out=t[:], in_=enc_t[:, i, a * width:(a + 1) * width])
-            raw[("enc", i, a)] = t
+            t = keep.tile([P, width], BF16, name="enc_raw%d_%d" % (i, part))
+            nc.sync.dma_start(out=t[:], in_=enc_rows[:, i, part * width:(part + 1) * width])
+            raw[("enc", i, part)] = t
+
+        def load_enc_quads(m):
+            t = keep.tile([P, 4, 8, P], BF16, name="enc_quads%d" % m)
+            for s in range(4):
+                for q in (0, 2, 1, 3):
+                    nc.sync.dma_start(out=t[QUAD * q:QUAD * (q + 1), s], in_=enc_quads[q, s, :, 8 * m:8 * (m + 1), :])
+            raw[("quads", m)] = t
 
         def load_enc_w(g):
             t = keep.tile([P, 2 * F], U8, name="enc_w%d" % g, align_bytes=64)
@@ -70,138 +91,131 @@ def tile_text_image_bridge_s3_kernel(
 
         def load_clip(m):
             t = keep.tile([P, 2 * C], BF16, name="clip_raw%d" % m)
-            nc.sync.dma_start(out=t[:], in_=clip_t[:, 2 * m * C:2 * (m + 1) * C])
+            nc.sync.dma_start(out=t[:], in_=clip_rows[:, 2 * m * C:2 * (m + 1) * C])
             raw[("clip", m)] = t
 
-        def load_plane(plane, scales):
+        def load_w_clip(h):
+            t = keep.tile([P, 4, BANK], BF16, name="w_clip_raw%d" % h)
+            nc.sync.dma_start(out=t[:], in_=w_clip_rows[:, :, h * BANK:(h + 1) * BANK])
+            raw[("w_clip", h)] = t
+
+        def load_plane(plane, scales, queue):
             for q in range(4):
-                nc.sync.dma_start(
-                    out=plane[32 * q:32 * q + 4].bitcast(I32),
+                queue.dma_start(
+                    out=plane[QUAD * q:QUAD * q + 4].bitcast(I32),
                     in_=scales[:, 4 * q:4 * q + 4, :].rearrange("g r n -> r g n").bitcast(I32),
                 )
 
-        enc_w = []
         load_enc(0, 0, 2)
         load_enc(1, 0, 2)
-        load_plane(enc_planes[0], enc_scales[0:2])
+        load_plane(enc_planes[0], enc_scales[0:2], nc.sync)
         load_enc_w(0)
         load_enc_w(1)
         load_enc(2, 0, 2)
-        wc_raw = []
-        wc_src = w_clip.rearrange("(p j) n -> p j n", j=4)
-
-        def load_wc(h):
-            t = keep.tile([P, 4, BANK], BF16, name="wc_raw%d" % h)
-            nc.sync.dma_start(out=t[:], in_=wc_src[:, :, h * BANK:(h + 1) * BANK])
-            wc_raw.append(t)
-
         load_enc(0, 1, 2)
-        load_wc(0)
+        load_w_clip(0)
         load_enc(1, 1, 2)
         load_enc(2, 1, 2)
-        load_plane(enc_planes[1], enc_scales[2:4])
+        load_plane(enc_planes[1], enc_scales[2:4], nc.sync)
         load_enc_w(2)
         load_enc_w(3)
         load_clip(0)
         load_clip(1)
-        load_wc(1)
+        load_w_clip(1)
         load_enc(3, 0, 1)
-        late_src = enc.rearrange("t (g y) -> (t g) y", g=4).rearrange("(s r j) (q k) -> q s r j k", s=4, j=4 * TILES, q=4)
-
-        def load_late(m):
-            t = keep.tile([P, 4, 8, P], BF16, name="late_raw%d" % m)
-            for s in range(4):
-                for q in (0, 2, 1, 3):
-                    nc.sync.dma_start(out=t[32 * q:32 * (q + 1), s], in_=late_src[q, s, :, 8 * m:8 * (m + 1), :])
-            raw[("late", m)] = t
-
         load_clip(2)
-        load_late(2)
-        load_plane(kv_plane[:, 0], key_scales)
-        load_plane(kv_plane[:, 1], val_scales)
-        kv_w = []
+        load_enc_quads(2)
         for m, words in enumerate((key_words, val_words)):
-            t = keep.tile([P, 2, 2 * D], U8, name="kv_w%d" % m, align_bytes=64)
+            t = keep.tile([P, 2, 2 * D], U8, name="out_w%d" % m, align_bytes=64)
             nc.sync.dma_start(out=t[:].bitcast(I32), in_=words.rearrange("g p b -> p g b").bitcast(I32))
-            kv_w.append(t)
+            out_w.append(t)
+        load_plane(val_plane, val_scales, nc.sync)
         load_clip(3)
-        load_late(3)
+        load_enc_quads(3)
 
-        bias_col = keep.tile([P, 8], F32, name="bias_col")
-        nc.gpsimd.tensor_copy(out=bias_col[:], in_=bias_raw[:].rearrange("p g t -> p (g t)"))
+        bias_cols = keep.tile([P, 8], F32, name="bias_cols")
+        nc.gpsimd.tensor_copy(out=bias_cols[:], in_=bias_raw[:].rearrange("p h t -> p (h t)"))
         emph = keep.tile([P, TILES], F32, name="emph")
         bias_rows = keep.tile([P, 2, BANK], F32, name="bias_rows")
 
-        srt = {}
-        banks = {}
-        grouped = {}
-        quant = {}
-        acc = {}
-        ctxs = {}
+        sorted_pairs = {}
+        turned = {}
+        woven = {}
+        quantised = {}
+        sums = {}
+        contexts = {}
 
-        def sort_words(key, src, tag, engine_copy=nc.vector.tensor_copy):
-            words = src.shape[1] // 2
-            t = work.tile([P, 2, words // 2], F32, name=tag, tag=tag, bufs=4, align_bytes=64)
+        def sort(key, engine_copy, tag="sorted_unit"):
+            src = raw[key]
+            t = work.tile([P, 2, src.shape[1] // 4], F32, name=tag, tag=tag, bufs=SORTED_BUFS, align_bytes=64)
             engine_copy(
                 out=t[:].rearrange("p u (j i) -> p j u i", i=4),
                 in_=src[:].bitcast(F32).rearrange("p (j i u) -> p j u i", i=4, u=2),
             )
-            srt[key] = t
+            sorted_pairs[key] = t
 
-        def turn(key, b, pieces):
+        def turn(key, b, block):
             t = bank(b)
             for u in range(2):
                 for c in range(2):
                     col = (2 * u + c) * P
-                    nc.tensor.transpose(t[:, col:col + P], pieces(u, c), ident[:])
-            banks[key] = t
+                    nc.tensor.transpose(t[:, col:col + P], block(u, c), ident[:])
+            turned[key] = t
 
-        def turn_enc(i, a, b):
-            if ("enc", i, a) in srt:
-                s, off = srt[("enc", i, a)], 0
-            else:
-                s, off = srt[("enc", i, 0)], 2 * a
-            turn(("enc", i, a), b, lambda u, c: s[:, u, (off + c) * P:(off + c + 1) * P])
+        def turn_unit(key, b):
+            s = sorted_pairs[key]
+            turn(key, b, lambda u, c: s[:, u, c * P:(c + 1) * P])
 
-        def turn_clip(m, b):
-            s = srt[("clip", m)]
-            turn(("clip", m), b, lambda u, c: s[:, u, c * P:(c + 1) * P])
-
-        def sort_late(i, a, engine_copy):
-            t = work.tile([P, 2, 2, 4, 32], F32, name="srt_half", tag="srt_half", bufs=4, align_bytes=64)
-            first = 4 * (i % 2) + 2 * a
-            src = raw[("late", i // 2)][:, :, first:first + 2, :].bitcast(F32)
-            engine_copy(
-                out=t[:].rearrange("p u c s j -> p s c u j"),
-                in_=src.rearrange("p s c (j u) -> p s c u j", u=2),
-            )
-            srt[("enc", i, a)] = t
-
-        def turn_late(i, a):
-            t = work.tile([P, BANK], F32, name="turned", tag="turned", align_bytes=64)
-            nc.vector.transpose(t[:], srt[("enc", i, a)][:].rearrange("p u c s j -> p (u c s j)"))
-            banks[("enc", i, a)] = t
-            empty(("enc", i, a))
-
-        def empty(key):
-            t = work.tile([P, 1024], BF16, name="grouped", tag="grouped", bufs=8, align_bytes=64)
-            nc.scalar.copy(
+        def weave(key):
+            t = work.tile([P, UNIT], BF16, name="woven", tag="woven", bufs=WOVEN_BUFS, align_bytes=64)
+            scalar_copy(
                 out=t[:].bitcast(F32).rearrange("p (c u) -> p c u", u=2),
-                in_=banks[key][:].rearrange("p (u c) -> p c u", u=2),
+                in_=turned[key][:].rearrange("p (u c) -> p c u", u=2),
             )
-            grouped[key] = t
+            woven[key] = t
 
-        def quantize(key):
-            src = grouped[key]
+        def turn_and_weave(*keys):
+            for b, key in enumerate(keys):
+                turn_unit(key, TURN0 + b)
+                weave(key)
+
+        def sort_quads(i):
+            for a in range(2):
+                t = work.tile([P, 2, 2, 4, QUAD], F32, name="sorted_unit", tag="sorted_unit",
+                              bufs=SORTED_BUFS, align_bytes=64)
+                first = 4 * (i % 2) + 2 * a
+                src = raw[("quads", i // 2)][:, :, first:first + 2, :].bitcast(F32)
+                vector_copy(
+                    out=t[:].rearrange("p u c s j -> p s c u j"),
+                    in_=src.rearrange("p s c (j u) -> p s c u j", u=2),
+                )
+                sorted_pairs[("enc", i, a)] = t
+
+        def turn_quads_and_weave(i, a):
+            t = work.tile([P, BANK], F32, name="turned", tag="turned", align_bytes=64)
+            nc.vector.transpose(t[:], sorted_pairs[("enc", i, a)][:].rearrange("p u c s j -> p (u c s j)"))
+            turned[("enc", i, a)] = t
+            weave(("enc", i, a))
+
+        def weave_w_clip(h):
+            t = keep.tile([P, 4 * BANK], BF16, name="w_clip_woven%d" % h, align_bytes=64)
+            vector_copy(
+                out=t[:].rearrange("p (c i t) -> p c t i", i=4, t=4),
+                in_=raw[("w_clip", h)][:].rearrange("p t (c i) -> p c t i", i=4),
+            )
+            woven[("w_clip", h)] = t
+
+        def quantize(*key):
+            src = woven[key]
             cols = src.shape[1] // 4
             name = "_".join([str(x) for x in key])
             codes = keep.tile([P, cols], U32, name="codes_" + name, align_bytes=64)
             scales = keep.tile([P, cols], U8, name="scales_" + name, align_bytes=64)
             nc.vector.quantize_mx(out=codes[:].bitcast(FP8X4), scales=scales[:], in_=src[:])
-            quant[key] = (codes, scales)
+            quantised[key] = (codes, scales)
 
         def mx(out, key, c, rhs, rhs_scale, start, stop):
-            codes, scales = quant[key]
+            codes, scales = quantised[key]
             nc.tensor.matmul_mx(
                 out=out[:], lhsT=codes[:, c * P:(c + 1) * P].bitcast(FP8X4),
                 lhsT_scale=scales[:, c * P:(c + 1) * P],
@@ -209,266 +223,236 @@ def tile_text_image_bridge_s3_kernel(
             )
 
         def enc_pass(i, h, g):
-            mx(acc[(i, h)], ("enc", i, g // 2), g % 2,
+            mx(sums[(i, h)], ("enc", i, g // 2), g % 2,
                enc_w[g][:, 2 * h * BANK:2 * (h + 1) * BANK].bitcast(FP4X4),
                enc_planes[g // 2][:, g % 2, h * BANK:(h + 1) * BANK], g == 0, False)
 
         def clip_pass(i, h):
-            codes, scales = quant[("wc", h)]
-            mx(acc[(i, h)], ("clip", i // 2), i % 2, codes[:].bitcast(FP8X4), scales[:], False, True)
+            codes, scales = quantised[("w_clip", h)]
+            mx(sums[(i, h)], ("clip", i // 2), i % 2, codes[:].bitcast(FP8X4), scales[:], False, True)
 
-        def stage1(i, h, b):
-            acc[(i, h)] = bank(b)
+        def head_passes(i, passes):
+            for g in passes:
+                for h in range(2):
+                    if g == 0:
+                        sums[(i, h)] = bank(HEAD_BANKS[i][h])
+                    enc_pass(i, h, g)
+
+        def stage1(i, h):
+            sums[(i, h)] = bank(CTX0 + h)
             for g in range(4):
                 enc_pass(i, h, g)
             clip_pass(i, h)
 
         def add_bias(i, h):
             if h == 0:
-                ctxs[i] = work.tile([P, F], BF16, name="ctx", tag="ctx", bufs=5)
+                contexts[i] = work.tile([P, F], BF16, name="context", tag="context", bufs=CONTEXT_BUFS)
             nc.vector.tensor_tensor(
-                out=ctxs[i][:, h * BANK:(h + 1) * BANK].rearrange("p (u j e) -> p u j e", u=2, e=2),
-                in0=acc[(i, h)][:].rearrange("p (j u e) -> p u j e", u=2, e=2),
+                out=contexts[i][:, h * BANK:(h + 1) * BANK].rearrange("p (u j e) -> p u j e", u=2, e=2),
+                in0=sums[(i, h)][:].rearrange("p (j u e) -> p u j e", u=2, e=2),
                 in1=bias_rows[:, h, :].rearrange("p (u j e) -> p u j e", u=2, e=2),
                 op=ALU.add,
             )
 
-        def turn_ctx(i, b):
-            w = ctxs[i][:].bitcast(F32)
-            turn(("ctx", i), b, lambda u, c: w[:, (2 * c + u) * P:(2 * c + u + 1) * P])
+        def turn_context(i, b):
+            pairs = contexts[i][:].bitcast(F32)
+            turn(("ctx", i), b, lambda u, c: pairs[:, (2 * c + u) * P:(2 * c + u + 1) * P])
 
-        def relu(i):
-            t = work.tile([P, 1024], BF16, name="grouped", tag="grouped", bufs=8, align_bytes=64)
+        def relu_and_weave(i):
+            t = work.tile([P, UNIT], BF16, name="woven", tag="woven", bufs=WOVEN_BUFS, align_bytes=64)
             nc.scalar.activation(
                 out=t[:].rearrange("p (c u e) -> p c u e", u=2, e=2),
-                in_=banks[("ctx", i)][:].bitcast(BF16).rearrange("p (u c e) -> p c u e", u=2, e=2),
+                in_=turned[("ctx", i)][:].bitcast(BF16).rearrange("p (u c e) -> p c u e", u=2, e=2),
                 func=ACT.Relu,
             )
-            grouped[("ctx", i)] = t
+            woven[("ctx", i)] = t
 
-        def stage2(i, m, b):
+        def stage2(i, m, b, operand):
             t = bank(b)
             for g in range(2):
-                mx(t, ("ctx", i), g, kv_w[m][:, g, :].bitcast(FP4X4), kv_plane[:, m, g, :], g == 0, g == 1)
-            acc[("out", i, m)] = t
+                key, c = operand(g)
+                mx(t, key, c, out_w[m][:, g, :].bitcast(FP4X4), out_planes[m][:, g, :], g == 0, g == 1)
+            sums[("out", i, m)] = t
 
-        def store(i, m, on_vector=False):
-            t = work.tile([P, D], F32, name="res", tag="res", bufs=8)
-            src = acc[("out", i, m)]
+        def store(i, m, values_on_vector=False):
+            t = work.tile([P, D], F32, name="result", tag="result", bufs=RESULT_BUFS)
+            src = sums[("out", i, m)]
             if m == 0:
-                nc.scalar.copy(out=t[:], in_=src[:])
-            elif on_vector:
+                scalar_copy(out=t[:], in_=src[:])
+            elif values_on_vector:
                 nc.vector.tensor_scalar(out=t[:], in0=src[:], scalar1=emph[:, i:i + 1], scalar2=None, op0=ALU.mult)
             else:
                 nc.scalar.activation(out=t[:], in_=src[:], func=ACT.Copy, scale=emph[:, i:i + 1])
             nc.sync.dma_start(out=outs[m][:, i, :], in_=t[:])
 
-        def interleave_wc(h, engine_copy):
-            t = keep.tile([P, 4 * BANK], BF16, name="wc_grouped%d" % h, align_bytes=64)
-            engine_copy(
-                out=t[:].rearrange("p (c i t) -> p c t i", i=4, t=4),
-                in_=wc_raw[h][:].rearrange("p t (c i) -> p c t i", i=4),
-            )
-            grouped[("wc", h)] = t
+        def stage2_and_store(i):
+            for m in range(2):
+                stage2(i, m, OUT0 + m, lambda g: (("ctx", i), g))
+                store(i, m)
 
-        T0, T1, T2, TC, A0, A1, B0, B1 = range(8)
-
-        head_banks = [(T2, TC), (A0, A1), (B0, B1)]
-
-        def sort_half(i, a):
-            sort_words(("enc", i, a), raw[("enc", i, a)], "srt_half")
-
-        def turn_pair(first, second):
-            for b, (i, a) in enumerate((first, second)):
-                turn_enc(i, a, T0 + b)
-                empty(("enc", i, a))
-
-        def head_passes(i, a):
-            if a == 0:
-                for h in range(2):
-                    acc[(i, h)] = bank(head_banks[i][h])
-            for g in range(2 * a, 2 * a + 2):
-                for h in range(2):
-                    enc_pass(i, h, g)
-
-        sort_half(0, 0)
-        sort_half(1, 0)
-        turn_pair((0, 0), (1, 0))
-        for g in range(2):
-            t = bank(B0 + g)
-            for s in range(4):
-                col = bias_col[:, 4 * g + s:4 * g + s + 1]
-                nc.tensor.transpose(t[:, s * P:(s + 1) * P], col.to_broadcast([P, P]), ident[:])
-            nc.scalar.copy(
-                out=bias_rows[:, g, :].rearrange("p (u j e) -> p u j e", u=2, e=2),
+        sort(("enc", 0, 0), vector_copy)
+        sort(("enc", 1, 0), vector_copy)
+        turn_and_weave(("enc", 0, 0), ("enc", 1, 0))
+        for h in range(2):
+            t = bank(OUT0 + h)
+            for slot in range(4):
+                col = bias_cols[:, 4 * h + slot:4 * h + slot + 1]
+                nc.tensor.transpose(t[:, slot * P:(slot + 1) * P], col.to_broadcast([P, P]), ident[:])
+            scalar_copy(
+                out=bias_rows[:, h, :].rearrange("p (u j e) -> p u j e", u=2, e=2),
                 in_=t[:].rearrange("p (u e j) -> p u j e", u=2, e=2),
             )
         nc.scalar.activation(out=emph[:], in_=emph_raw[:], func=ACT.Copy)
-        quantize(("enc", 0, 0))
-        quantize(("enc", 1, 0))
-        head_passes(0, 0)
-        sort_half(2, 0)
-        sort_half(0, 1)
-        turn_pair((2, 0), (0, 1))
-        head_passes(1, 0)
-        interleave_wc(0, nc.vector.tensor_copy)
-        sort_half(1, 1)
-        sort_half(2, 1)
-        quantize(("enc", 2, 0))
-        quantize(("enc", 0, 1))
-        turn_pair((1, 1), (2, 1))
-        quantize(("wc", 0))
-        head_passes(2, 0)
-        head_passes(0, 1)
-        vcopy, scopy = nc.vector.tensor_copy, nc.scalar.copy
-        quantize(("enc", 1, 1))
-        sort_words(("clip", 0), raw[("clip", 0)], "srt_half")
-        quantize(("enc", 2, 1))
-        sort_words(("clip", 1), raw[("clip", 1)], "srt_half")
-        for m in range(2):
-            turn_clip(m, T0 + m)
-            empty(("clip", m))
-        head_passes(1, 1)
-        interleave_wc(1, vcopy)
-        sort_words(("enc", 3, 0), raw[("enc", 3, 0)], "srt", scopy)
-        quantize(("clip", 0))
-        quantize(("wc", 1))
-        quantize(("clip", 1))
-        for h in range(2):
-            enc_pass(2, h, 2)
+        quantize("enc", 0, 0)
+        quantize("enc", 1, 0)
+        head_passes(0, (0, 1))
+        sort(("enc", 2, 0), vector_copy)
+        sort(("enc", 0, 1), vector_copy)
+        turn_and_weave(("enc", 2, 0), ("enc", 0, 1))
+        head_passes(1, (0, 1))
+        weave_w_clip(0)
+        sort(("enc", 1, 1), vector_copy)
+        sort(("enc", 2, 1), vector_copy)
+        quantize("enc", 2, 0)
+        quantize("enc", 0, 1)
+        turn_and_weave(("enc", 1, 1), ("enc", 2, 1))
+        quantize("w_clip", 0)
+        head_passes(2, (0, 1))
+        head_passes(0, (2, 3))
+        quantize("enc", 1, 1)
+        sort(("clip", 0), vector_copy)
+        quantize("enc", 2, 1)
+        sort(("clip", 1), vector_copy)
+        turn_and_weave(("clip", 0), ("clip", 1))
+        head_passes(1, (2, 3))
+        weave_w_clip(1)
+        sort(("enc", 3, 0), scalar_copy, "sorted_tile")
+        quantize("clip", 0)
+        quantize("w_clip", 1)
+        quantize("clip", 1)
+        nc.vector.memset(key_plane[:].bitcast(I32), 0)
+        load_plane(key_plane, key_scales, nc.gpsimd)
+        head_passes(2, (2,))
         clip_pass(0, 0)
         clip_pass(1, 0)
-        turn_pair((3, 0), (3, 1))
+        whole = sorted_pairs[("enc", 3, 0)]
+        for a in range(2):
+            turn(("enc", 3, a), TURN0 + a, lambda u, c: whole[:, u, (2 * a + c) * P:(2 * a + c + 1) * P])
+            weave(("enc", 3, a))
         clip_pass(0, 1)
         clip_pass(1, 1)
-        for h in range(2):
-            enc_pass(2, h, 3)
+        head_passes(2, (3,))
         clip_pass(2, 0)
         clip_pass(2, 1)
         add_bias(0, 0)
         add_bias(1, 0)
         add_bias(0, 1)
-        quantize(("enc", 3, 0))
-        quantize(("enc", 3, 1))
+        quantize("enc", 3, 0)
+        quantize("enc", 3, 1)
         add_bias(1, 1)
-        sort_words(("clip", 2), raw[("clip", 2)], "srt_half", scopy)
-        sort_late(4, 0, scopy)
-        sort_late(4, 1, scopy)
-        stage1(3, 0, A0)
-        turn_ctx(0, TC)
-        relu(0)
-        turn_clip(2, T2)
-        turn_ctx(1, T0)
+        sort(("clip", 2), scalar_copy)
+
+        stage1(3, 0)
+        turn_context(0, TURN3)
+        relu_and_weave(0)
+        turn_unit(("clip", 2), TURN2)
+        turn_context(1, TURN0)
         add_bias(2, 0)
         add_bias(2, 1)
-        turn_late(4, 0)
-        turn_late(4, 1)
-        quantize(("ctx", 0))
-        empty(("clip", 2))
+        weave(("clip", 2))
+        sort_quads(4)
+        turn_quads_and_weave(4, 0)
+        turn_quads_and_weave(4, 1)
+        quantize("ctx", 0)
         add_bias(3, 0)
-        quantize(("enc", 4, 0))
-        quantize(("enc", 4, 1))
-        quantize(("clip", 2))
-        stage1(3, 1, A1)
+        quantize("enc", 4, 0)
+        quantize("enc", 4, 1)
+        quantize("clip", 2)
+        stage1(3, 1)
         add_bias(3, 1)
-        for m in range(2):
-            stage2(0, m, B0 + m)
-            store(0, m)
-        relu(1)
-        sort_late(5, 0, vcopy)
-        sort_late(5, 1, vcopy)
-        turn_late(5, 0)
-        quantize(("ctx", 1))
-        turn_late(5, 1)
-        sort_words(("clip", 3), raw[("clip", 3)], "srt_half")
-        stage1(4, 0, A0)
-        add_bias(4, 0)
-        stage1(4, 1, A1)
-        add_bias(4, 1)
-        quantize(("enc", 5, 0))
-        quantize(("enc", 5, 1))
-        for m in range(2):
-            stage2(1, m, B0 + m)
-            store(1, m)
-        turn_ctx(2, TC)
-        relu(2)
-        turn_clip(3, T2)
-        turn_ctx(3, T0)
-        turn_ctx(4, T1)
-        sort_late(6, 0, vcopy)
-        sort_late(6, 1, vcopy)
-        turn_late(6, 0)
-        turn_late(6, 1)
-        empty(("clip", 3))
-        relu(3)
-        quantize(("ctx", 2))
-        stage1(5, 0, A0)
-        add_bias(5, 0)
-        quantize(("enc", 6, 0))
-        quantize(("enc", 6, 1))
-        quantize(("clip", 3))
-        stage1(5, 1, A1)
-        add_bias(5, 1)
-        for m in range(2):
-            stage2(2, m, B0 + m)
-            store(2, m)
-        relu(4)
-        sort_late(7, 0, vcopy)
-        sort_late(7, 1, vcopy)
-        turn_late(7, 0)
-        quantize(("ctx", 3))
-        turn_late(7, 1)
-        stage1(6, 0, A0)
-        add_bias(6, 0)
-        stage1(6, 1, A1)
-        add_bias(6, 1)
-        quantize(("ctx", 4))
-        quantize(("enc", 7, 0))
-        quantize(("enc", 7, 1))
-        for m in range(2):
-            stage2(3, m, B0 + m)
-            store(3, m)
+        stage2_and_store(0)
 
-        n = TILES - 1
-        turn_ctx(n - 2, TC)
-        relu(n - 2)
-        turn_ctx(n - 1, T0)
-        relu(n - 1)
-        for m in range(2):
-            stage2(n - 3, m, B0 + m)
-            store(n - 3, m)
-        quantize(("ctx", n - 2))
-        stage1(n, 0, A0)
-        quantize(("ctx", n - 1))
-        add_bias(n, 0)
-        stage1(n, 1, A1)
-        add_bias(n, 1)
-        for m in range(2):
-            stage2(n - 2, m, B0 + m)
-        store(n - 2, 0)
-        store(n - 2, 1, True)
-        w = ctxs[n][:].bitcast(F32)
+        relu_and_weave(1)
+        sort_quads(5)
+        turn_quads_and_weave(5, 0)
+        quantize("ctx", 1)
+        turn_quads_and_weave(5, 1)
+        sort(("clip", 3), vector_copy)
         for h in range(2):
-            t = bank(T1 + h)
+            stage1(4, h)
+            add_bias(4, h)
+        quantize("enc", 5, 0)
+        quantize("enc", 5, 1)
+        stage2_and_store(1)
+
+        turn_context(2, TURN3)
+        relu_and_weave(2)
+        turn_unit(("clip", 3), TURN2)
+        turn_context(3, TURN0)
+        turn_context(4, TURN1)
+        sort_quads(6)
+        turn_quads_and_weave(6, 0)
+        turn_quads_and_weave(6, 1)
+        weave(("clip", 3))
+        relu_and_weave(3)
+        quantize("ctx", 2)
+        stage1(5, 0)
+        add_bias(5, 0)
+        quantize("enc", 6, 0)
+        quantize("enc", 6, 1)
+        quantize("clip", 3)
+        stage1(5, 1)
+        add_bias(5, 1)
+        stage2_and_store(2)
+
+        relu_and_weave(4)
+        sort_quads(7)
+        turn_quads_and_weave(7, 0)
+        quantize("ctx", 3)
+        turn_quads_and_weave(7, 1)
+        for h in range(2):
+            stage1(6, h)
+            add_bias(6, h)
+        quantize("ctx", 4)
+        quantize("enc", 7, 0)
+        quantize("enc", 7, 1)
+        stage2_and_store(3)
+
+        last = TILES - 1
+        for i, b in ((last - 2, TURN3), (last - 1, TURN0)):
+            turn_context(i, b)
+            relu_and_weave(i)
+        stage2_and_store(last - 3)
+        quantize("ctx", last - 2)
+        stage1(last, 0)
+        quantize("ctx", last - 1)
+        add_bias(last, 0)
+        stage1(last, 1)
+        add_bias(last, 1)
+        for m in range(2):
+            stage2(last - 2, m, OUT0 + m, lambda g: (("ctx", last - 2), g))
+        store(last - 2, 0)
+        store(last - 2, 1, values_on_vector=True)
+        pairs = contexts[last][:].bitcast(F32)
+        for g in range(2):
+            t = bank(TURN1 + g)
             for u in range(2):
-                nc.tensor.transpose(t[:, u * P:(u + 1) * P], w[:, (2 * h + u) * P:(2 * h + u + 1) * P], ident[:])
-            half = keep.tile([P, 512], BF16, name="last%d" % h, align_bytes=64)
+                nc.tensor.transpose(t[:, u * P:(u + 1) * P], pairs[:, (2 * g + u) * P:(2 * g + u + 1) * P], ident[:])
+            half = keep.tile([P, UNIT // 2], BF16, name="last_woven%d" % g, align_bytes=64)
             dst = half[:].rearrange("p (c u e) -> p c u e", u=2, e=2)
             src = t[:, 0:2 * P].bitcast(BF16).rearrange("p (u c e) -> p c u e", u=2, e=2)
-            if h == 0:
+            if g == 0:
                 nc.scalar.activation(out=dst, in_=src, func=ACT.Relu)
             else:
                 nc.vector.tensor_scalar(out=dst, in0=src, scalar1=0.0, scalar2=None, op0=ALU.max)
-            grouped[("last", h)] = half
+            woven[("last", g)] = half
+        for m, b in enumerate((TURN3, TURN0)):
+            stage2(last - 1, m, b, lambda g: (("ctx", last - 1), g))
+        quantize("last", 0)
+        quantize("last", 1)
+        store(last - 1, 0)
+        store(last - 1, 1, values_on_vector=True)
         for m in range(2):
-            stage2(n - 1, m, (TC, T0)[m])
-        quantize(("last", 0))
-        quantize(("last", 1))
-        store(n - 1, 0)
-        store(n - 1, 1, True)
-        for m in range(2):
-            acc[("out", n, m)] = bank(A0 + m)
-            for g in range(2):
-                mx(acc[("out", n, m)], ("last", g), 0, kv_w[m][:, g, :].bitcast(FP4X4), kv_plane[:, m, g, :], g == 0, g == 1)
-        store(n, 0)
-        store(n, 1, True)
+            stage2(last, m, CTX0 + m, lambda g: (("last", g), 0))
+        store(last, 0)
+        store(last, 1, values_on_vector=True)

from contextlib import ExitStack

import concourse.mybir as mybir
from concourse.masks import make_identity

T, C, E, F, D = 1024, 512, 2048, 1024, 512
FLOPS = 2 * T * F * (C + E) + 2 * 2 * T * F * D

F32 = mybir.dt.float32
BF16 = mybir.dt.bfloat16
I32 = mybir.dt.int32
U32 = mybir.dt.uint32
U8 = mybir.dt.uint8
FP8X4 = mybir.dt.float8_e4m3fn_x4
FP4X4 = mybir.dt.float4_e2m1fn_x4
ACT = mybir.ActivationFunctionType
ALU = mybir.AluOpType

P = 128
TILES = T // P
BANK = 512
UNIT = 2 * BANK
QUAD = 32

TURN0, TURN1, TURN2, TURN3, CTX0, CTX1, OUT0, OUT1 = range(8)
HEAD_BANKS = ((TURN2, TURN3), (CTX0, CTX1), (OUT0, OUT1))

SORTED_BUFS, TURNED_BUFS, WOVEN_BUFS, CONTEXT_BUFS, RESULT_BUFS = 4, 3, 8, 5, 8


def tile_text_image_bridge_s3_kernel(
    tc, clip, enc, w_clip, enc_words, enc_scales, bias, key_words, key_scales,
    val_words, val_scales, emphasis, out_0, out_1,
):
    nc = tc.nc
    vector_copy, scalar_copy = nc.vector.tensor_copy, nc.scalar.copy
    enc_rows = enc.rearrange("(p i) k -> p i k", i=TILES)
    enc_quads = enc.rearrange("t (g y) -> (t g) y", g=4).rearrange(
        "(s r j) (q k) -> q s r j k", s=4, j=4 * TILES, q=4)
    clip_rows = clip.rearrange("(p i) k -> p (i k)", i=TILES)
    w_clip_rows = w_clip.rearrange("(p t) n -> p t n", t=4)
    outs = [o.rearrange("(p i) d -> p i d", i=TILES) for o in (out_0, out_1)]

    with ExitStack() as stack:
        keep = stack.enter_context(tc.tile_pool(name="keep", bufs=1))
        work = stack.enter_context(tc.tile_pool(name="work", bufs=TURNED_BUFS))
        psum = stack.enter_context(tc.psum_pool(name="psum", bufs=1))
        stack.enter_context(tc.manual_schedule())

        def bank(b):
            return psum.tile([P, BANK], F32, name="bank%d" % b, tag="bank%d" % b)

        enc_planes = []
        for a in range(2):
            plane = keep.tile([P, 2, F], U8, name="enc_plane%d" % a, align_bytes=64)
            nc.vector.memset(plane[:].bitcast(I32), 0)
            enc_planes.append(plane)
        val_plane = keep.tile([P, 2, D], U8, name="val_plane", align_bytes=64)
        nc.vector.memset(val_plane[:].bitcast(I32), 0)
        key_plane = keep.tile([P, 2, D], U8, name="key_plane", align_bytes=64)
        out_planes = (key_plane, val_plane)

        ident = keep.tile([P, P], F32, name="ident")
        make_identity(nc, ident[:])
        bias_raw = keep.tile([P, 2, 4], BF16, name="bias_raw")
        nc.gpsimd.dma_start(out=bias_raw[:], in_=bias.rearrange("(h j t) -> j h t", h=2, t=4))
        emph_raw = keep.tile([P, TILES], BF16, name="emph_raw")
        nc.gpsimd.dma_start(out=emph_raw[:], in_=emphasis.rearrange("(p i) -> p i", i=TILES))

        raw = {}
        enc_w = []
        out_w = []

        def load_enc(i, part, parts):
            width = E // parts
            t = keep.tile([P, width], BF16, name="enc_raw%d_%d" % (i, part))
            nc.sync.dma_start(out=t[:], in_=enc_rows[:, i, part * width:(part + 1) * width])
            raw[("enc", i, part)] = t

        def load_enc_quads(m):
            t = keep.tile([P, 4, 8, P], BF16, name="enc_quads%d" % m)
            for s in range(4):
                for q in (0, 2, 1, 3):
                    nc.sync.dma_start(out=t[QUAD * q:QUAD * (q + 1), s], in_=enc_quads[q, s, :, 8 * m:8 * (m + 1), :])
            raw[("quads", m)] = t

        def load_enc_w(g):
            t = keep.tile([P, 2 * F], U8, name="enc_w%d" % g, align_bytes=64)
            nc.sync.dma_start(out=t[:].bitcast(I32), in_=enc_words[g].bitcast(I32))
            enc_w.append(t)

        def load_clip(m):
            t = keep.tile([P, 2 * C], BF16, name="clip_raw%d" % m)
            nc.sync.dma_start(out=t[:], in_=clip_rows[:, 2 * m * C:2 * (m + 1) * C])
            raw[("clip", m)] = t

        def load_w_clip(h):
            t = keep.tile([P, 4, BANK], BF16, name="w_clip_raw%d" % h)
            nc.sync.dma_start(out=t[:], in_=w_clip_rows[:, :, h * BANK:(h + 1) * BANK])
            raw[("w_clip", h)] = t

        def load_plane(plane, scales, queue):
            for q in range(4):
                queue.dma_start(
                    out=plane[QUAD * q:QUAD * q + 4].bitcast(I32),
                    in_=scales[:, 4 * q:4 * q + 4, :].rearrange("g r n -> r g n").bitcast(I32),
                )

        load_enc(0, 0, 2)
        load_enc(1, 0, 2)
        load_plane(enc_planes[0], enc_scales[0:2], nc.sync)
        load_enc_w(0)
        load_enc_w(1)
        load_enc(2, 0, 2)
        load_enc(0, 1, 2)
        load_w_clip(0)
        load_enc(1, 1, 2)
        load_enc(2, 1, 2)
        load_plane(enc_planes[1], enc_scales[2:4], nc.sync)
        load_enc_w(2)
        load_enc_w(3)
        load_clip(0)
        load_clip(1)
        load_w_clip(1)
        load_enc(3, 0, 1)
        load_clip(2)
        load_enc_quads(2)
        for m, words in enumerate((key_words, val_words)):
            t = keep.tile([P, 2, 2 * D], U8, name="out_w%d" % m, align_bytes=64)
            nc.sync.dma_start(out=t[:].bitcast(I32), in_=words.rearrange("g p b -> p g b").bitcast(I32))
            out_w.append(t)
        load_plane(val_plane, val_scales, nc.sync)
        load_clip(3)
        load_enc_quads(3)

        bias_cols = keep.tile([P, 8], F32, name="bias_cols")
        nc.gpsimd.tensor_copy(out=bias_cols[:], in_=bias_raw[:].rearrange("p h t -> p (h t)"))
        emph = keep.tile([P, TILES], F32, name="emph")
        bias_rows = keep.tile([P, 2, BANK], F32, name="bias_rows")

        sorted_pairs = {}
        turned = {}
        woven = {}
        quantised = {}
        sums = {}
        contexts = {}

        def sort(key, engine_copy, tag="sorted_unit"):
            src = raw[key]
            t = work.tile([P, 2, src.shape[1] // 4], F32, name=tag, tag=tag, bufs=SORTED_BUFS, align_bytes=64)
            engine_copy(
                out=t[:].rearrange("p u (j i) -> p j u i", i=4),
                in_=src[:].bitcast(F32).rearrange("p (j i u) -> p j u i", i=4, u=2),
            )
            sorted_pairs[key] = t

        def turn(key, b, block):
            t = bank(b)
            for u in range(2):
                for c in range(2):
                    col = (2 * u + c) * P
                    nc.tensor.transpose(t[:, col:col + P], block(u, c), ident[:])
            turned[key] = t

        def turn_unit(key, b):
            s = sorted_pairs[key]
            turn(key, b, lambda u, c: s[:, u, c * P:(c + 1) * P])

        def weave(key):
            t = work.tile([P, UNIT], BF16, name="woven", tag="woven", bufs=WOVEN_BUFS, align_bytes=64)
            scalar_copy(
                out=t[:].bitcast(F32).rearrange("p (c u) -> p c u", u=2),
                in_=turned[key][:].rearrange("p (u c) -> p c u", u=2),
            )
            woven[key] = t

        def turn_and_weave(*keys):
            for b, key in enumerate(keys):
                turn_unit(key, TURN0 + b)
                weave(key)

        def sort_quads(i):
            for a in range(2):
                t = work.tile([P, 2, 2, 4, QUAD], F32, name="sorted_unit", tag="sorted_unit",
                              bufs=SORTED_BUFS, align_bytes=64)
                first = 4 * (i % 2) + 2 * a
                src = raw[("quads", i // 2)][:, :, first:first + 2, :].bitcast(F32)
                vector_copy(
                    out=t[:].rearrange("p u c s j -> p s c u j"),
                    in_=src.rearrange("p s c (j u) -> p s c u j", u=2),
                )
                sorted_pairs[("enc", i, a)] = t

        def turn_quads_and_weave(i, a):
            t = work.tile([P, BANK], F32, name="turned", tag="turned", align_bytes=64)
            nc.vector.transpose(t[:], sorted_pairs[("enc", i, a)][:].rearrange("p u c s j -> p (u c s j)"))
            turned[("enc", i, a)] = t
            weave(("enc", i, a))

        def weave_w_clip(h):
            t = keep.tile([P, 4 * BANK], BF16, name="w_clip_woven%d" % h, align_bytes=64)
            vector_copy(
                out=t[:].rearrange("p (c i t) -> p c t i", i=4, t=4),
                in_=raw[("w_clip", h)][:].rearrange("p t (c i) -> p c t i", i=4),
            )
            woven[("w_clip", h)] = t

        def quantize(*key):
            src = woven[key]
            cols = src.shape[1] // 4
            name = "_".join([str(x) for x in key])
            codes = keep.tile([P, cols], U32, name="codes_" + name, align_bytes=64)
            scales = keep.tile([P, cols], U8, name="scales_" + name, align_bytes=64)
            nc.vector.quantize_mx(out=codes[:].bitcast(FP8X4), scales=scales[:], in_=src[:])
            quantised[key] = (codes, scales)

        def mx(out, key, c, rhs, rhs_scale, start, stop):
            codes, scales = quantised[key]
            nc.tensor.matmul_mx(
                out=out[:], lhsT=codes[:, c * P:(c + 1) * P].bitcast(FP8X4),
                lhsT_scale=scales[:, c * P:(c + 1) * P],
                rhs=rhs, rhs_scale=rhs_scale, start=start, stop=stop,
            )

        def enc_pass(i, h, g):
            mx(sums[(i, h)], ("enc", i, g // 2), g % 2,
               enc_w[g][:, 2 * h * BANK:2 * (h + 1) * BANK].bitcast(FP4X4),
               enc_planes[g // 2][:, g % 2, h * BANK:(h + 1) * BANK], g == 0, False)

        def clip_pass(i, h):
            codes, scales = quantised[("w_clip", h)]
            mx(sums[(i, h)], ("clip", i // 2), i % 2, codes[:].bitcast(FP8X4), scales[:], False, True)

        def head_passes(i, passes):
            for g in passes:
                for h in range(2):
                    if g == 0:
                        sums[(i, h)] = bank(HEAD_BANKS[i][h])
                    enc_pass(i, h, g)

        def stage1(i, h):
            sums[(i, h)] = bank(CTX0 + h)
            for g in range(4):
                enc_pass(i, h, g)
            clip_pass(i, h)

        def add_bias(i, h):
            if h == 0:
                contexts[i] = work.tile([P, F], BF16, name="context", tag="context", bufs=CONTEXT_BUFS)
            nc.vector.tensor_tensor(
                out=contexts[i][:, h * BANK:(h + 1) * BANK].rearrange("p (u j e) -> p u j e", u=2, e=2),
                in0=sums[(i, h)][:].rearrange("p (j u e) -> p u j e", u=2, e=2),
                in1=bias_rows[:, h, :].rearrange("p (u j e) -> p u j e", u=2, e=2),
                op=ALU.add,
            )

        def turn_context(i, b):
            pairs = contexts[i][:].bitcast(F32)
            turn(("ctx", i), b, lambda u, c: pairs[:, (2 * c + u) * P:(2 * c + u + 1) * P])

        def relu_and_weave(i):
            t = work.tile([P, UNIT], BF16, name="woven", tag="woven", bufs=WOVEN_BUFS, align_bytes=64)
            nc.scalar.activation(
                out=t[:].rearrange("p (c u e) -> p c u e", u=2, e=2),
                in_=turned[("ctx", i)][:].bitcast(BF16).rearrange("p (u c e) -> p c u e", u=2, e=2),
                func=ACT.Relu,
            )
            woven[("ctx", i)] = t

        def stage2(i, m, b, operand):
            t = bank(b)
            for g in range(2):
                key, c = operand(g)
                mx(t, key, c, out_w[m][:, g, :].bitcast(FP4X4), out_planes[m][:, g, :], g == 0, g == 1)
            sums[("out", i, m)] = t

        def store(i, m, values_on_vector=False):
            t = work.tile([P, D], F32, name="result", tag="result", bufs=RESULT_BUFS)
            src = sums[("out", i, m)]
            if m == 0:
                scalar_copy(out=t[:], in_=src[:])
            elif values_on_vector:
                nc.vector.tensor_scalar(out=t[:], in0=src[:], scalar1=emph[:, i:i + 1], scalar2=None, op0=ALU.mult)
            else:
                nc.scalar.activation(out=t[:], in_=src[:], func=ACT.Copy, scale=emph[:, i:i + 1])
            nc.sync.dma_start(out=outs[m][:, i, :], in_=t[:])

        def stage2_and_store(i):
            for m in range(2):
                stage2(i, m, OUT0 + m, lambda g: (("ctx", i), g))
                store(i, m)

        sort(("enc", 0, 0), vector_copy)
        sort(("enc", 1, 0), vector_copy)
        turn_and_weave(("enc", 0, 0), ("enc", 1, 0))
        for h in range(2):
            t = bank(OUT0 + h)
            for slot in range(4):
                col = bias_cols[:, 4 * h + slot:4 * h + slot + 1]
                nc.tensor.transpose(t[:, slot * P:(slot + 1) * P], col.to_broadcast([P, P]), ident[:])
            scalar_copy(
                out=bias_rows[:, h, :].rearrange("p (u j e) -> p u j e", u=2, e=2),
                in_=t[:].rearrange("p (u e j) -> p u j e", u=2, e=2),
            )
        nc.scalar.activation(out=emph[:], in_=emph_raw[:], func=ACT.Copy)
        quantize("enc", 0, 0)
        quantize("enc", 1, 0)
        head_passes(0, (0, 1))
        sort(("enc", 2, 0), vector_copy)
        sort(("enc", 0, 1), vector_copy)
        turn_and_weave(("enc", 2, 0), ("enc", 0, 1))
        head_passes(1, (0, 1))
        weave_w_clip(0)
        sort(("enc", 1, 1), vector_copy)
        sort(("enc", 2, 1), vector_copy)
        quantize("enc", 2, 0)
        quantize("enc", 0, 1)
        turn_and_weave(("enc", 1, 1), ("enc", 2, 1))
        quantize("w_clip", 0)
        head_passes(2, (0, 1))
        head_passes(0, (2, 3))
        quantize("enc", 1, 1)
        sort(("clip", 0), vector_copy)
        quantize("enc", 2, 1)
        sort(("clip", 1), vector_copy)
        turn_and_weave(("clip", 0), ("clip", 1))
        head_passes(1, (2, 3))
        weave_w_clip(1)
        sort(("enc", 3, 0), scalar_copy, "sorted_tile")
        quantize("clip", 0)
        quantize("w_clip", 1)
        quantize("clip", 1)
        nc.vector.memset(key_plane[:].bitcast(I32), 0)
        load_plane(key_plane, key_scales, nc.gpsimd)
        head_passes(2, (2,))
        clip_pass(0, 0)
        clip_pass(1, 0)
        whole = sorted_pairs[("enc", 3, 0)]
        for a in range(2):
            turn(("enc", 3, a), TURN0 + a, lambda u, c: whole[:, u, (2 * a + c) * P:(2 * a + c + 1) * P])
            weave(("enc", 3, a))
        clip_pass(0, 1)
        clip_pass(1, 1)
        head_passes(2, (3,))
        clip_pass(2, 0)
        clip_pass(2, 1)
        add_bias(0, 0)
        add_bias(1, 0)
        add_bias(0, 1)
        quantize("enc", 3, 0)
        quantize("enc", 3, 1)
        add_bias(1, 1)
        sort(("clip", 2), scalar_copy)

        stage1(3, 0)
        turn_context(0, TURN3)
        relu_and_weave(0)
        turn_unit(("clip", 2), TURN2)
        turn_context(1, TURN0)
        add_bias(2, 0)
        add_bias(2, 1)
        weave(("clip", 2))
        sort_quads(4)
        turn_quads_and_weave(4, 0)
        turn_quads_and_weave(4, 1)
        quantize("ctx", 0)
        add_bias(3, 0)
        quantize("enc", 4, 0)
        quantize("enc", 4, 1)
        quantize("clip", 2)
        stage1(3, 1)
        add_bias(3, 1)
        stage2_and_store(0)

        relu_and_weave(1)
        sort_quads(5)
        turn_quads_and_weave(5, 0)
        quantize("ctx", 1)
        turn_quads_and_weave(5, 1)
        sort(("clip", 3), vector_copy)
        for h in range(2):
            stage1(4, h)
            add_bias(4, h)
        quantize("enc", 5, 0)
        quantize("enc", 5, 1)
        stage2_and_store(1)

        turn_context(2, TURN3)
        relu_and_weave(2)
        turn_unit(("clip", 3), TURN2)
        turn_context(3, TURN0)
        turn_context(4, TURN1)
        sort_quads(6)
        turn_quads_and_weave(6, 0)
        turn_quads_and_weave(6, 1)
        weave(("clip", 3))
        relu_and_weave(3)
        quantize("ctx", 2)
        stage1(5, 0)
        add_bias(5, 0)
        quantize("enc", 6, 0)
        quantize("enc", 6, 1)
        quantize("clip", 3)
        stage1(5, 1)
        add_bias(5, 1)
        stage2_and_store(2)

        relu_and_weave(4)
        sort_quads(7)
        turn_quads_and_weave(7, 0)
        quantize("ctx", 3)
        turn_quads_and_weave(7, 1)
        for h in range(2):
            stage1(6, h)
            add_bias(6, h)
        quantize("ctx", 4)
        quantize("enc", 7, 0)
        quantize("enc", 7, 1)
        stage2_and_store(3)

        last = TILES - 1
        for i, b in ((last - 2, TURN3), (last - 1, TURN0)):
            turn_context(i, b)
            relu_and_weave(i)
        stage2_and_store(last - 3)
        quantize("ctx", last - 2)
        stage1(last, 0)
        quantize("ctx", last - 1)
        add_bias(last, 0)
        stage1(last, 1)
        add_bias(last, 1)
        for m in range(2):
            stage2(last - 2, m, OUT0 + m, lambda g: (("ctx", last - 2), g))
        store(last - 2, 0)
        store(last - 2, 1, values_on_vector=True)
        pairs = contexts[last][:].bitcast(F32)
        for g in range(2):
            t = bank(TURN1 + g)
            for u in range(2):
                nc.tensor.transpose(t[:, u * P:(u + 1) * P], pairs[:, (2 * g + u) * P:(2 * g + u + 1) * P], ident[:])
            half = keep.tile([P, UNIT // 2], BF16, name="last_woven%d" % g, align_bytes=64)
            dst = half[:].rearrange("p (c u e) -> p c u e", u=2, e=2)
            src = t[:, 0:2 * P].bitcast(BF16).rearrange("p (u c e) -> p c u e", u=2, e=2)
            if g == 0:
                nc.scalar.activation(out=dst, in_=src, func=ACT.Relu)
            else:
                nc.vector.tensor_scalar(out=dst, in0=src, scalar1=0.0, scalar2=None, op0=ALU.max)
            woven[("last", g)] = half
        for m, b in enumerate((TURN3, TURN0)):
            stage2(last - 1, m, b, lambda g: (("ctx", last - 1), g))
        quantize("last", 0)
        quantize("last", 1)
        store(last - 1, 0)
        store(last - 1, 1, values_on_vector=True)
        for m in range(2):
            stage2(last, m, CTX0 + m, lambda g: (("last", g), 0))
        store(last, 0)
        store(last, 1, values_on_vector=True)
